import numpy as np
import ml_dtypes


def mxq(x, axis, fmt="e4m3"):
    dtype, down = {"e4m3": (ml_dtypes.float8_e4m3fn, 7), "e5m2": (ml_dtypes.float8_e5m2, 14)}[fmt]
    v = np.moveaxis(np.asarray(x, np.float32).astype(ml_dtypes.bfloat16).astype(np.float64), axis, -1)
    blocks = v.reshape(v.shape[:-1] + (-1, 32))
    amax = np.abs(blocks).max(-1, keepdims=True)
    byte = np.maximum(np.where(amax > 0, np.frexp(amax)[1] - 1 + 127, 0) - down, 1)
    scale = np.exp2(byte - 127.0)
    codes = (blocks / scale).astype(np.float32).astype(dtype).astype(np.float64)
    return np.moveaxis((codes * scale).reshape(v.shape), -1, axis)


WIDE = False


def mx_kscale(k):
    if not WIDE:
        return np.ones(k)
    levels = np.array([10, -10, 5, -5, 0])
    if k % 512:
        return np.exp2(np.random.permutation(np.resize(levels, k // 32))).repeat(32)
    a = np.empty((k // 512, 16))
    for p in range(k // 512):
        a[p, :8] = np.random.permutation(np.resize(levels, 8))
        for g in range(8):
            far = levels[np.abs(levels - a[p, g]) >= 10]
            a[p, g + 8] = far[np.random.randint(len(far))]
    return np.exp2(a.ravel()).repeat(32)


BF16 = ml_dtypes.bfloat16


def bf(x):
    return np.asarray(x, np.float32).astype(BF16)


def f64(x):
    return np.asarray(x).astype(np.float64)


T, N, D, R, F, E = 2048, 2048, 512, 512, 1024, 512

EPS = 1e-5


def pair_features(a):
    return np.concatenate([np.exp(a), np.exp(-a)], axis=1)


def setup_inputs():
    u, s, t = mx_kscale(D), mx_kscale(T), mx_kscale(F)
    return {"key_proj": bf(np.random.standard_normal((T, R))),
            "token_weight": bf(np.random.uniform(0.25, 0.75, T) / np.sqrt(T) * s),
            "key_gain": bf((1 + 0.1 * np.random.standard_normal(F)) * t),
            "value": bf(np.random.standard_normal((T, E)) / s[:, None]),
            "state": bf(np.random.standard_normal((F, E)) * t[:, None]),
            "decay": bf(np.random.uniform(0.5, 1.0, F)),
            "query": bf(np.random.standard_normal((N, D)) * u),
            "omega": bf(np.random.standard_normal((D, R)) / np.sqrt(D) / u[:, None]),
            "read_weight": bf(np.random.standard_normal(F) / np.sqrt(F) / t),
            "norm_gain": bf(1 + 0.1 * np.random.standard_normal(E))}


def reference(key_proj, token_weight, key_gain, value, state, decay, query, omega, read_weight, norm_gain):
    pk = pair_features(f64(key_proj)) * f64(token_weight)[:, None] * f64(key_gain)
    fresh = mxq(pk, 0, "e4m3").T @ mxq(f64(value), 0, "e4m3")
    st = f64(decay)[:, None] * f64(state) + fresh
    a = mxq(f64(query), 1, "e4m3") @ mxq(f64(omega), 0, "e4m3")
    pq = pair_features(a) * f64(read_weight)
    o = mxq(pq, 1, "e4m3") @ mxq(st, 0, "e4m3")
    return o / np.sqrt(np.mean(np.square(o), axis=1, keepdims=True) + EPS) * f64(norm_gain)

@@ -1,0 +1,418 @@
+from contextlib import ExitStack
+
+import concourse.mybir as mybir
+from concourse.masks import make_identity
+
+T, N, D, R, F, E = 2048, 2048, 512, 512, 1024, 512
+EPS = 1e-5
+FLOPS = 2 * T * F * E + 2 * N * D * R + 2 * N * F * E
+
+F32 = mybir.dt.float32
+BF16 = mybir.dt.bfloat16
+U32 = mybir.dt.uint32
+U8 = mybir.dt.uint8
+FP8X4 = mybir.dt.float8_e4m3fn_x4
+ALU = mybir.AluOpType
+ACT = mybir.ActivationFunctionType
+
+P = 128
+PACK = 4
+W = 512
+TOKEN_PASSES = T // W
+HALVES = F // W
+GROUPS = N // W
+STEPS = HALVES * TOKEN_PASSES
+LN_LOW = 2.0 ** -63
+LN_HIGH = 2.0 ** 63
+QUERY_LAG = 2
+FRESH_LAG = 2
+VECTOR_PQ_TILES = 2
+MIX_AHEAD = 10
+Q_AHEAD = 5
+
+
+def tile_paired_exp_state_read_f4_kernel(
+    tc, key_proj, token_weight, key_gain, value, state, decay, query, omega, read_weight, norm_gain, out
+):
+    nc = tc.nc
+    with ExitStack() as ctx:
+        keep = ctx.enter_context(tc.tile_pool(name="keep", bufs=1))
+        work = ctx.enter_context(tc.tile_pool(name="work", bufs=1))
+        psum = ctx.enter_context(tc.psum_pool(name="psum", bufs=1))
+        ctx.enter_context(tc.manual_schedule())
+
+        def load_rows(name, rows):
+            t = keep.tile([P, PACK, W], BF16, name=name, align_bytes=64)
+            nc.sync.dma_start(out=t[:], in_=rows.rearrange("(p j) w -> p j w", j=PACK))
+            return t
+
+        def block(src, i):
+            return src[i * W : (i + 1) * W, :]
+
+        n_tw = TOKEN_PASSES * PACK
+        n_rw = HALVES * PACK
+        n_w = n_tw + n_rw
+        weights = keep.tile([P, 32], BF16, name="weights")
+        gain_cols = keep.tile([P, n_rw], BF16, name="gain_cols")
+        decay_cols = keep.tile([P, n_rw], BF16, name="decay_cols")
+        nc.sync.dma_start(
+            out=weights[:, 0:n_tw].rearrange("p (c j) -> p c j", j=PACK),
+            in_=token_weight.rearrange("(c p j) -> p c j", p=P, j=PACK),
+        )
+        nc.sync.dma_start(
+            out=weights[:, n_tw:n_w].rearrange("p (g t) -> p g t", t=PACK),
+            in_=read_weight.rearrange("(g p t) -> p g t", p=P, t=PACK),
+        )
+        nc.sync.dma_start(
+            out=gain_cols[:].rearrange("p (g t) -> p g t", t=PACK),
+            in_=key_gain.rearrange("(g p t) -> p g t", p=P, t=PACK),
+        )
+        keys, values, queries, states = {}, {}, {}, {}
+        values[0] = load_rows("value0", block(value, 0))
+        keys[0] = load_rows("key0", block(key_proj, 0))
+        omega_rows = load_rows("omega_rows", omega)
+        queries[0] = load_rows("query0", block(query, 0))
+        for c in range(1, TOKEN_PASSES):
+            keys[c] = load_rows("key%d" % c, block(key_proj, c))
+            values[c] = load_rows("value%d" % c, block(value, c))
+            queries[c] = load_rows("query%d" % c, block(query, c))
+        nc.sync.dma_start(
+            out=decay_cols[:].rearrange("p (g t) -> p g t", t=PACK),
+            in_=decay.rearrange("(g p t) -> p g t", p=P, t=PACK),
+        )
+        for g in range(HALVES):
+            states[g] = load_rows("state%d" % g, block(state, g))
+        gain_row = keep.tile([P, E], BF16, name="gain_row")
+        nc.sync.dma_start(out=gain_row[:], in_=norm_gain.partition_broadcast(P))
+
+        warm = keep.tile([P, 1], F32, name="warm")
+        nc.vector.memset(warm[:], 1.0)
+        warm_out = keep.tile([P, 1], F32, name="warm_out")
+        nc.scalar.activation(out=warm_out[:], in_=warm[:], func=ACT.Ln)
+        ident_f32 = keep.tile([P, P], F32, name="ident_f32")
+        make_identity(nc, ident_f32[:])
+        ident_bf16 = keep.tile([P, P], BF16, name="ident_bf16")
+        make_identity(nc, ident_bf16[:])
+
+        minus_half = keep.tile([P, 2], F32, name="minus_half")
+        nc.gpsimd.memset(minus_half[:], -0.5)
+
+        w_in = weights[:, 0:n_w]
+        mag = keep.tile([P, n_w], F32, name="mag")
+        half_sign = keep.tile([P, n_w], F32, name="half_sign")
+        low = keep.tile([P, n_w], F32, name="low")
+        high = keep.tile([P, n_w], F32, name="high")
+        ln_args = keep.tile([P, 2, n_w], F32, name="ln_args")
+        ln_parts = keep.tile([P, 2, n_w], F32, name="ln_parts")
+        ln_w = keep.tile([P, n_w], F32, name="ln_w")
+        nc.vector.scalar_tensor_tensor(out=mag[:], in0=w_in, scalar=-1.0, in1=w_in, op0=ALU.mult, op1=ALU.max)
+        nc.vector.tensor_scalar(
+            out=half_sign[:], in0=w_in, scalar1=0.0, scalar2=0.5, op0=ALU.is_ge, op1=ALU.subtract
+        )
+        nc.vector.tensor_scalar(out=low[:], in0=mag[:], scalar1=LN_LOW, scalar2=LN_HIGH, op0=ALU.min, op1=ALU.mult)
+        nc.vector.tensor_scalar(out=high[:], in0=mag[:], scalar1=LN_HIGH, scalar2=LN_LOW, op0=ALU.max, op1=ALU.mult)
+        nc.vector.tensor_scalar(
+            out=ln_args[:, 0, :], in0=mag[:], scalar1=LN_LOW, scalar2=LN_HIGH, op0=ALU.max, op1=ALU.min
+        )
+        nc.vector.scalar_tensor_tensor(
+            out=ln_args[:, 1, :], in0=low[:], scalar=LN_LOW, in1=high[:], op0=ALU.max, op1=ALU.mult
+        )
+        nc.scalar.activation(out=ln_parts[:], in_=ln_args[:], func=ACT.Ln)
+        signed_gain = keep.tile([P, n_rw], BF16, name="signed_gain")
+        nc.vector.scalar_tensor_tensor(
+            out=signed_gain[:], in0=half_sign[:, n_tw:n_w], scalar=2.0, in1=gain_cols[:], op0=ALU.mult, op1=ALU.mult
+        )
+        nc.vector.tensor_tensor(out=ln_w[:], in0=ln_parts[:, 0, :], in1=ln_parts[:, 1, :], op=ALU.add)
+        gain_bank = psum.tile([P, F], BF16, tag="gain", name="gain_bank")
+        for i in range(n_rw):
+            nc.tensor.transpose(
+                gain_bank[:, i * P : (i + 1) * P], signed_gain[:, i : i + 1].to_broadcast([P, P]), ident_bf16[:]
+            )
+
+        def new_grouped():
+            return work.tile([P, W * PACK], BF16, tag="grouped", name="grouped", bufs=5, align_bytes=64)
+
+        def interleave(rows):
+            grouped = new_grouped()
+            nc.vector.tensor_copy(
+                out=grouped[:].rearrange("p (c i j) -> p c j i", i=4, j=PACK),
+                in_=rows[:].rearrange("p j (c i) -> p c j i", i=4),
+            )
+            return grouped
+
+        def interleave_half_on_tensor(rows, grouped, h, tag):
+            bank = psum.tile([P, 2 * W], BF16, tag=tag, name="mix_bank")
+            for k in range(2):
+                cols = slice((2 * h + k) * P, (2 * h + k + 1) * P)
+                nc.tensor.matmul(
+                    bank[:, k * W : (k + 1) * W].rearrange("p (w j) -> p w j", j=PACK),
+                    lhsT=ident_bf16[:],
+                    rhs=rows[:, :, cols].rearrange("p j w -> p w j"),
+                    start=True,
+                    stop=True,
+                )
+            nc.scalar.copy(out=grouped[:, h * 2 * W : (h + 1) * 2 * W], in_=bank[:])
+
+        def quantize(grouped, tag, bufs):
+            codes = work.tile([P, W], U32, tag=tag + "_codes", name=tag + "_codes", bufs=bufs, align_bytes=64)
+            scales = work.tile([P, W], U8, tag=tag + "_scales", name=tag + "_scales", bufs=bufs, align_bytes=64)
+            nc.vector.quantize_mx(out=codes[:].bitcast(FP8X4), scales=scales[:], in_=grouped[:])
+            return codes, scales
+
+        def mx(acc, stationary, col, moving, start, stop):
+            cols = slice(col * P, (col + 1) * P)
+            nc.tensor.matmul_mx(
+                out=acc,
+                lhsT=stationary[0][:, cols].bitcast(FP8X4),
+                lhsT_scale=stationary[1][:, cols],
+                rhs=moving[0][:].bitcast(FP8X4),
+                rhs_scale=moving[1][:],
+                start=start,
+                stop=stop,
+            )
+
+        def sign_value(c):
+            for j in range(PACK):
+                col = c * PACK + j
+                nc.vector.tensor_scalar(
+                    out=values[c][:, j, :], in0=values[c][:, j, :], scalar1=half_sign[:, col : col + 1],
+                    scalar2=2.0, op0=ALU.mult, op1=ALU.mult,
+                )
+
+        def key_exps(s):
+            g, c = divmod(s, TOKEN_PASSES)
+            feats = work.tile([P, PACK, W], F32, tag="key_feats", name="key_feats", bufs=3)
+            for j in range(PACK):
+                col = c * PACK + j
+                nc.scalar.activation(
+                    out=feats[:, j, :].rearrange("p (t m) -> p t m", t=PACK),
+                    in_=keys[c][:, j, :].rearrange("p (m t) -> p t m", t=PACK),
+                    func=ACT.Exp, scale=1.0 - 2.0 * g, bias=ln_w[:, col : col + 1],
+                )
+            return feats
+
+        def key_gain_mul(s, feats):
+            g = s // TOKEN_PASSES
+            grouped = new_grouped()
+            gains = gain_bank[:, g * W : (g + 1) * W].rearrange("p (c i) -> p c i", i=4)
+            nc.vector.tensor_tensor(
+                out=grouped[:].rearrange("p (c i j) -> p c j i", i=4, j=PACK),
+                in0=feats[:].rearrange("p j (c i) -> p c j i", i=4),
+                in1=gains.unsqueeze(2).to_broadcast([P, W // 4, PACK, 4]),
+                op=ALU.mult,
+            )
+            return grouped
+
+        fresh = {}
+
+        def fresh_matmuls(s):
+            g, c = divmod(s, TOKEN_PASSES)
+            for t in range(PACK):
+                if c == 0:
+                    fresh[g, t] = psum.tile([P, E], F32, tag="acc%d" % t, name="fresh")
+                mx(fresh[g, t][:], pk_mx[s], t, value_mx[c], c == 0, c == TOKEN_PASSES - 1)
+
+        query_grouped = {}
+
+        def query_transposes(i, tag="turn"):
+            n, h = divmod(i, 2)
+            if h == 0:
+                query_grouped[n] = work.tile(
+                    [P, W * PACK], BF16, tag="query_grouped", name="query_grouped", bufs=2, align_bytes=64
+                )
+            bank = psum.tile([P, 2, 2, P], F32, tag=tag, name="turn_bank")
+            for b in range(2):
+                words = queries[n][:, 2 * h + b, :].bitcast(F32)
+                for u in range(2):
+                    nc.tensor.transpose(bank[:, b, u, :], words[:, u : 2 * P : 2], ident_f32[:])
+            return bank
+
+        def query_copy(i, bank):
+            n, h = divmod(i, 2)
+            dst = query_grouped[n][:, h * 2 * W : (h + 1) * 2 * W].bitcast(F32)
+            nc.scalar.copy(
+                out=dst.rearrange("p (b r u) -> p b r u", b=2, u=2), in_=bank[:].rearrange("p b u r -> p b r u")
+            )
+
+        pq_rows = {}
+
+        def project(i):
+            n, h = divmod(i, 2)
+            banks = []
+            for k in range(2):
+                bank = psum.tile([P, W], F32, tag="proj%d" % k, name="proj_bank")
+                mx(bank[:], omega_mx, 2 * h + k, query_mx[n], True, True)
+                banks.append(bank)
+            return banks
+
+        def query_exps(i, banks):
+            n, h = divmod(i, 2)
+            if h == 0:
+                for g in range(HALVES):
+                    pq_rows[n, g] = work.tile([P, PACK, W], BF16, tag="pq_rows", name="pq_rows", bufs=8)
+            for k in range(2):
+                t = 2 * h + k
+                for g in range(HALVES):
+                    col = n_tw + g * PACK + t
+                    nc.scalar.activation(
+                        out=pq_rows[n, g][:, t, :], in_=banks[k][:], func=ACT.Exp,
+                        scale=1.0 - 2.0 * g, bias=ln_w[:, col : col + 1],
+                    )
+
+        def state_rows(g):
+            rows = work.tile([P, PACK, E], BF16, tag="state_rows", name="state_rows", bufs=2)
+            for t in range(PACK):
+                col = g * PACK + t
+                nc.vector.scalar_tensor_tensor(
+                    out=rows[:, t, :], in0=states[g][:, t, :], scalar=signed_decay[:, col : col + 1],
+                    in1=fresh[g, t][:], op0=ALU.mult, op1=ALU.add,
+                )
+            return rows
+
+        pk_mx, value_mx, query_mx, pq_mx, state_mx = {}, {}, {}, {}, {}
+
+        sign_value(0)
+        omega_grouped = new_grouped()
+        value_grouped = interleave(values[0])
+        nc.vector.tensor_copy(
+            out=omega_grouped[:].rearrange("p (t m j) -> p t m j", t=PACK, j=PACK),
+            in_=omega_rows[:].rearrange("p j (m t) -> p t m j", t=PACK),
+        )
+        value_mx[0] = quantize(value_grouped, "value", TOKEN_PASSES)
+        omega_mx = quantize(omega_grouped, "omega", 1)
+        signed_decay = keep.tile([P, n_rw], F32, name="signed_decay")
+
+        pq_order = [(n, g) for n in range(GROUPS) for g in range(HALVES)]
+        vector_keys = [(0, 0), (1, 1), (2, 1), (3, 1)][:VECTOR_PQ_TILES]
+        mix_list = [(key, h) for key in pq_order if key not in vector_keys for h in range(2)]
+        mix_tags = ["turn", "proj0", "proj1"]
+        spare_tags = ["value%d" % c for c in range(TOKEN_PASSES)] + ["query%d" % n for n in range(GROUPS)]
+        mixed = {}
+
+        def mix(i):
+            key, h = mix_list[i]
+            if h == 0:
+                mixed[key] = keep.tile([P, W * PACK], BF16, tag=spare_tags[i // 2], name="mixed", align_bytes=64)
+            interleave_half_on_tensor(pq_rows[key], mixed[key], h, mix_tags[i % (3 if i < MIX_AHEAD else 2)])
+
+        def quantize_pq(key):
+            pq_mx[key] = quantize(mixed[key], "pq", 8)
+
+        key_grouped = {}
+        first_bank = query_transposes(0, "proj0")
+        for s in range(STEPS):
+            q = s - QUERY_LAG
+            if q >= 0:
+                proj_banks = project(q)
+            if s + 1 < STEPS:
+                turn_bank = query_transposes(s + 1)
+            if s >= FRESH_LAG:
+                fresh_matmuls(s - FRESH_LAG)
+            feats = key_exps(s)
+            if s == 0:
+                query_copy(0, first_bank)
+            if s + 1 < STEPS:
+                query_copy(s + 1, turn_bank)
+            if q >= 0:
+                query_exps(q, proj_banks)
+            update = s - FRESH_LAG == TOKEN_PASSES - 1
+            more_values = s + 1 < TOKEN_PASSES
+            if update:
+                nc.vector.scalar_tensor_tensor(
+                    out=signed_decay[:], in0=half_sign[:, n_tw:n_w], scalar=2.0, in1=decay_cols[:],
+                    op0=ALU.mult, op1=ALU.mult,
+                )
+            key_grouped[s] = key_gain_mul(s, feats)
+            if more_values:
+                sign_value(s + 1)
+            if update:
+                rows = state_rows(0)
+            if 1 <= s < TOKEN_PASSES:
+                value_mx[s] = quantize(value_grouped, "value", TOKEN_PASSES)
+            if s - FRESH_LAG == TOKEN_PASSES:
+                state_mx[0] = quantize(state_grouped, "state", HALVES)
+            if s >= 1:
+                pk_mx[s - 1] = quantize(key_grouped[s - 1], "pk", 4)
+            if s % 2 == 0:
+                query_mx[s // 2] = quantize(query_grouped[s // 2], "query", 2)
+            if more_values:
+                value_grouped = interleave(values[s + 1])
+            if update:
+                state_grouped = interleave(rows)
+
+        for q in range(STEPS - QUERY_LAG, STEPS):
+            proj_banks = project(q)
+            if q == STEPS - QUERY_LAG:
+                for s in range(STEPS - FRESH_LAG, STEPS - 1):
+                    fresh_matmuls(s)
+            query_exps(q, proj_banks)
+        mixed[0, 0] = interleave(pq_rows[0, 0])
+        pk_mx[STEPS - 1] = quantize(key_grouped[STEPS - 1], "pk", 4)
+        mix(0)
+        fresh_matmuls(STEPS - 1)
+        mixed[1, 1] = interleave(pq_rows[1, 1])
+        for i in range(1, MIX_AHEAD):
+            mix(i)
+        rows = state_rows(1)
+        quantize_pq(pq_order[0])
+        state_grouped = interleave(rows)
+        quantize_pq(pq_order[1])
+        state_mx[1] = quantize(state_grouped, "state", HALVES)
+
+        out_tags = ["acc0", "acc1", "acc2", "acc3", "gain", "proj1"]
+        sums = keep.tile([P, 2 * GROUPS * 2], F32, name="sums")
+        mean_sq = keep.tile([P, 2 * GROUPS * 2], F32, name="mean_sq")
+        inv_rms = keep.tile([P, 2 * GROUPS * 2], F32, name="inv_rms")
+
+        def read(k):
+            n, h = divmod(k, 2)
+            banks = []
+            for b in range(2):
+                bank = psum.tile([P, E], F32, tag=out_tags[(2 * k + b) % len(out_tags)], name="read_bank")
+                for g in range(HALVES):
+                    mx(bank[:], pq_mx[n, g], 2 * h + b, state_mx[g], g == 0, g == HALVES - 1)
+                banks.append(bank)
+            return banks
+
+        def square_sums(k, banks):
+            for b in range(2):
+                squares = work.tile([P, E], BF16, tag="squares", name="squares", bufs=2)
+                col = 2 * k + b
+                nc.scalar.activation(
+                    out=squares[:], in_=banks[b][:], func=ACT.Square, accum_out=sums[:, col : col + 1]
+                )
+
+        def inverse_rms(k):
+            cols = slice(2 * k, 2 * k + 2)
+            nc.gpsimd.tensor_scalar(
+                out=mean_sq[:, cols], in0=sums[:, cols], scalar1=1.0 / E, scalar2=EPS, op0=ALU.mult, op1=ALU.add
+            )
+            nc.gpsimd.tensor_tensor(out=inv_rms[:, cols], in0=mean_sq[:, cols], in1=minus_half[:], op=ALU.pow)
+
+        def finish(k, banks):
+            n, h = divmod(k, 2)
+            rows = out[n * W : (n + 1) * W, :].rearrange("(p b) e -> p b e", b=PACK)
+            for b in range(2):
+                col = 2 * k + b
+                result = work.tile([P, E], F32, tag="result", name="result", bufs=8)
+                nc.vector.scalar_tensor_tensor(
+                    out=result[:], in0=banks[b][:], scalar=inv_rms[:, col : col + 1], in1=gain_row[:],
+                    op0=ALU.mult, op1=ALU.mult,
+                )
+                nc.sync.dma_start(out=rows[:, 2 * h + b, :], in_=result[:])
+
+        pairs = 2 * GROUPS
+        read_banks = {}
+        for k in range(pairs + 1):
+            if k < pairs:
+                read_banks[k] = read(k)
+                square_sums(k, read_banks[k])
+                inverse_rms(k)
+                for i in range(MIX_AHEAD + 2 * k, min(MIX_AHEAD + 2 * k + 2, len(mix_list))):
+                    mix(i)
+                if 0 < k and k + 3 < pairs and pq_order[k + 3] in vector_keys:
+                    mixed[pq_order[k + 3]] = interleave(pq_rows[pq_order[k + 3]])
+                for i in range(2 if k == 0 else k + Q_AHEAD, min(k + Q_AHEAD + 1, pairs)):
+                    quantize_pq(pq_order[i])
+            if k >= 1:
+                finish(k - 1, read_banks[k - 1])

@@ -24,11 +24,11 @@ GROUPS = N // W
 STEPS = HALVES * TOKEN_PASSES
 LN_LOW = 2.0 ** -63
 LN_HIGH = 2.0 ** 63
-QUERY_LAG = 2
+QUERY_LAG = 3
 FRESH_LAG = 2
-VECTOR_PQ_TILES = 2
-MIX_AHEAD = 10
-Q_AHEAD = 5
+G_COLS = 384
+S_HALVES = 2
+EARLY_Q = 3
 
 
 def tile_paired_exp_state_read_f4_kernel(
@@ -94,9 +94,6 @@ def tile_paired_exp_state_read_f4_kernel(
         ident_bf16 = keep.tile([P, P], BF16, name="ident_bf16")
         make_identity(nc, ident_bf16[:])
 
-        minus_half = keep.tile([P, 2], F32, name="minus_half")
-        nc.gpsimd.memset(minus_half[:], -0.5)
-
         w_in = weights[:, 0:n_w]
         mag = keep.tile([P, n_w], F32, name="mag")
         half_sign = keep.tile([P, n_w], F32, name="half_sign")
@@ -130,28 +127,27 @@ def tile_paired_exp_state_read_f4_kernel(
             )
 
         def new_grouped():
-            return work.tile([P, W * PACK], BF16, tag="grouped", name="grouped", bufs=5, align_bytes=64)
+            return work.tile([P, W * PACK], BF16, tag="grouped", name="grouped", bufs=3, align_bytes=64)
 
-        def interleave(rows):
-            grouped = new_grouped()
+        def interleave(rows, grouped, first=0):
             nc.vector.tensor_copy(
-                out=grouped[:].rearrange("p (c i j) -> p c j i", i=4, j=PACK),
-                in_=rows[:].rearrange("p j (c i) -> p c j i", i=4),
+                out=grouped[:, first * PACK :].rearrange("p (c i j) -> p c j i", i=4, j=PACK),
+                in_=rows[:, :, first:].rearrange("p j (c i) -> p c j i", i=4),
             )
-            return grouped
 
-        def interleave_half_on_tensor(rows, grouped, h, tag):
-            bank = psum.tile([P, 2 * W], BF16, tag=tag, name="mix_bank")
-            for k in range(2):
-                cols = slice((2 * h + k) * P, (2 * h + k + 1) * P)
-                nc.tensor.matmul(
-                    bank[:, k * W : (k + 1) * W].rearrange("p (w j) -> p w j", j=PACK),
-                    lhsT=ident_bf16[:],
-                    rhs=rows[:, :, cols].rearrange("p j w -> p w j"),
-                    start=True,
-                    stop=True,
-                )
-            nc.scalar.copy(out=grouped[:, h * 2 * W : (h + 1) * 2 * W], in_=bank[:])
+        def interleave_on_gpsimd(rows, grouped, count):
+            nc.gpsimd.tensor_scalar(
+                out=grouped[:, : count * PACK].rearrange("p (w j) -> p w j", j=PACK),
+                in0=rows[:, :, :count].rearrange("p j w -> p w j"),
+                scalar1=1.0, scalar2=1.0, op0=ALU.mult, op1=ALU.mult,
+            )
+
+        def interleave_half_on_scalar(rows, grouped, h):
+            half = W // 2
+            nc.scalar.copy(
+                out=grouped[:, h * half * PACK : (h + 1) * half * PACK].rearrange("p (c i j) -> p c j i", i=4, j=PACK),
+                in_=rows[:, :, h * half : (h + 1) * half].rearrange("p j (c i) -> p c j i", i=4),
+            )
 
         def quantize(grouped, tag, bufs):
             codes = work.tile([P, W], U32, tag=tag + "_codes", name=tag + "_codes", bufs=bufs, align_bytes=64)
@@ -216,7 +212,7 @@ def tile_paired_exp_state_read_f4_kernel(
 
         def query_transposes(i, tag="turn"):
             n, h = divmod(i, 2)
-            if h == 0:
+            if n not in query_grouped:
                 query_grouped[n] = work.tile(
                     [P, W * PACK], BF16, tag="query_grouped", name="query_grouped", bufs=2, align_bytes=64
                 )
@@ -272,34 +268,25 @@ def tile_paired_exp_state_read_f4_kernel(
         pk_mx, value_mx, query_mx, pq_mx, state_mx = {}, {}, {}, {}, {}
 
         sign_value(0)
-        omega_grouped = new_grouped()
-        value_grouped = interleave(values[0])
-        nc.vector.tensor_copy(
-            out=omega_grouped[:].rearrange("p (t m j) -> p t m j", t=PACK, j=PACK),
-            in_=omega_rows[:].rearrange("p j (m t) -> p t m j", t=PACK),
-        )
-        value_mx[0] = quantize(value_grouped, "value", TOKEN_PASSES)
-        omega_mx = quantize(omega_grouped, "omega", 1)
+        value_grouped = new_grouped()
+        query_grouped[0] = new_grouped()
         signed_decay = keep.tile([P, n_rw], F32, name="signed_decay")
+        interleave(values[0], value_grouped)
+        value_mx[0] = quantize(value_grouped, "value", TOKEN_PASSES)
 
         pq_order = [(n, g) for n in range(GROUPS) for g in range(HALVES)]
-        vector_keys = [(0, 0), (1, 1), (2, 1), (3, 1)][:VECTOR_PQ_TILES]
-        mix_list = [(key, h) for key in pq_order if key not in vector_keys for h in range(2)]
-        mix_tags = ["turn", "proj0", "proj1"]
         spare_tags = ["value%d" % c for c in range(TOKEN_PASSES)] + ["query%d" % n for n in range(GROUPS)]
         mixed = {}
 
-        def mix(i):
-            key, h = mix_list[i]
-            if h == 0:
-                mixed[key] = keep.tile([P, W * PACK], BF16, tag=spare_tags[i // 2], name="mixed", align_bytes=64)
-            interleave_half_on_tensor(pq_rows[key], mixed[key], h, mix_tags[i % (3 if i < MIX_AHEAD else 2)])
+        def spare_grouped(key):
+            mixed[key] = keep.tile([P, W * PACK], BF16, tag=spare_tags.pop(0), name="mixed", align_bytes=64)
+            return mixed[key]
 
         def quantize_pq(key):
             pq_mx[key] = quantize(mixed[key], "pq", 8)
 
-        key_grouped = {}
         first_bank = query_transposes(0, "proj0")
+        side = rows = None
         for s in range(STEPS):
             q = s - QUERY_LAG
             if q >= 0:
@@ -316,52 +303,72 @@ def tile_paired_exp_state_read_f4_kernel(
             if q >= 0:
                 query_exps(q, proj_banks)
             update = s - FRESH_LAG == TOKEN_PASSES - 1
-            more_values = s + 1 < TOKEN_PASSES
-            if update:
+            key_grouped = key_gain_mul(s, feats)
+            previous_side = side
+            side = new_grouped()
+            if s == 0:
+                dst = side[:].rearrange("p (t m j) -> p t m j", t=PACK, j=PACK)
+                src = omega_rows[:].rearrange("p j (m t) -> p t m j", t=PACK)
+                nc.gpsimd.tensor_scalar(
+                    out=dst[:, :3], in0=src[:, :3], scalar1=1.0, scalar2=1.0, op0=ALU.mult, op1=ALU.mult
+                )
+                nc.vector.tensor_copy(out=dst[:, 3], in_=src[:, 3])
+            elif update:
+                interleave_on_gpsimd(pq_rows[0, 1], side, W)
+                rows = state_rows(0)
+            else:
+                side_rows = values[s] if s < TOKEN_PASSES else {4: pq_rows[0, 0], 6: rows, 7: pq_rows.get((1, 0))}[s]
+                interleave_on_gpsimd(side_rows, side, G_COLS)
+                interleave(side_rows, side, G_COLS)
+            if s == 1:
+                omega_mx = quantize(previous_side, "omega", 1)
+            elif 1 < s <= TOKEN_PASSES:
+                value_mx[s - 1] = quantize(previous_side, "value", TOKEN_PASSES)
+            elif s == 5:
+                pq_mx[0, 0] = quantize(previous_side, "pq", 8)
+            elif s == 6:
+                pq_mx[0, 1] = quantize(previous_side, "pq", 8)
+            elif s == 7:
+                state_mx[0] = quantize(previous_side, "state", HALVES)
+            if s % 2 == 0:
+                query_mx[s // 2] = quantize(query_grouped[s // 2], "query", 2)
+            if s + 1 < TOKEN_PASSES:
+                sign_value(s + 1)
+            if s == TOKEN_PASSES:
                 nc.vector.scalar_tensor_tensor(
                     out=signed_decay[:], in0=half_sign[:, n_tw:n_w], scalar=2.0, in1=decay_cols[:],
                     op0=ALU.mult, op1=ALU.mult,
                 )
-            key_grouped[s] = key_gain_mul(s, feats)
-            if more_values:
-                sign_value(s + 1)
-            if update:
-                rows = state_rows(0)
-            if 1 <= s < TOKEN_PASSES:
-                value_mx[s] = quantize(value_grouped, "value", TOKEN_PASSES)
-            if s - FRESH_LAG == TOKEN_PASSES:
-                state_mx[0] = quantize(state_grouped, "state", HALVES)
-            if s >= 1:
-                pk_mx[s - 1] = quantize(key_grouped[s - 1], "pk", 4)
-            if s % 2 == 0:
-                query_mx[s // 2] = quantize(query_grouped[s // 2], "query", 2)
-            if more_values:
-                value_grouped = interleave(values[s + 1])
-            if update:
-                state_grouped = interleave(rows)
+            pk_mx[s] = quantize(key_grouped, "pk", 4)
 
+        mixed[1, 0] = side
         for q in range(STEPS - QUERY_LAG, STEPS):
             proj_banks = project(q)
-            if q == STEPS - QUERY_LAG:
-                for s in range(STEPS - FRESH_LAG, STEPS - 1):
-                    fresh_matmuls(s)
+            if q + QUERY_LAG - FRESH_LAG < STEPS:
+                fresh_matmuls(q + QUERY_LAG - FRESH_LAG)
             query_exps(q, proj_banks)
-        mixed[0, 0] = interleave(pq_rows[0, 0])
-        pk_mx[STEPS - 1] = quantize(key_grouped[STEPS - 1], "pk", 4)
-        mix(0)
-        fresh_matmuls(STEPS - 1)
-        mixed[1, 1] = interleave(pq_rows[1, 1])
-        for i in range(1, MIX_AHEAD):
-            mix(i)
+        for key in [(1, 1), (2, 0), (2, 1)]:
+            mixed[key] = new_grouped()
+        interleave(pq_rows[1, 1], mixed[1, 1])
+        quantize_pq((1, 0))
+        interleave_on_gpsimd(pq_rows[2, 1], mixed[2, 1], G_COLS)
         rows = state_rows(1)
-        quantize_pq(pq_order[0])
-        state_grouped = interleave(rows)
-        quantize_pq(pq_order[1])
+        interleave(pq_rows[2, 1], mixed[2, 1], G_COLS)
+        state_grouped = spare_grouped("state")
+        interleave(rows, state_grouped)
+        quantize_pq((1, 1))
         state_mx[1] = quantize(state_grouped, "state", HALVES)
+        interleave(pq_rows[2, 0], mixed[2, 0])
+        for i, key in enumerate([(3, 0), (3, 1)]):
+            spare_grouped(key)
+            halves = min(2, max(0, S_HALVES - 2 * i))
+            for h in range(halves):
+                interleave_half_on_scalar(pq_rows[key], mixed[key], h)
+            if halves < 2:
+                interleave(pq_rows[key], mixed[key], halves * W // 2)
 
-        out_tags = ["acc0", "acc1", "acc2", "acc3", "gain", "proj1"]
+        out_tags = ["acc0", "acc1", "acc2", "acc3", "gain", "turn", "proj0", "proj1"]
         sums = keep.tile([P, 2 * GROUPS * 2], F32, name="sums")
-        mean_sq = keep.tile([P, 2 * GROUPS * 2], F32, name="mean_sq")
         inv_rms = keep.tile([P, 2 * GROUPS * 2], F32, name="inv_rms")
 
         def read(k):
@@ -374,20 +381,15 @@ def tile_paired_exp_state_read_f4_kernel(
                 banks.append(bank)
             return banks
 
-        def square_sums(k, banks):
-            for b in range(2):
-                squares = work.tile([P, E], BF16, tag="squares", name="squares", bufs=2)
-                col = 2 * k + b
-                nc.scalar.activation(
-                    out=squares[:], in_=banks[b][:], func=ACT.Square, accum_out=sums[:, col : col + 1]
-                )
+        def square_sum(col, bank):
+            squares = work.tile([P, E], BF16, tag="squares", name="squares", bufs=2)
+            nc.scalar.activation(out=squares[:], in_=bank[:], func=ACT.Square, accum_out=sums[:, col : col + 1])
 
         def inverse_rms(k):
-            cols = slice(2 * k, 2 * k + 2)
-            nc.gpsimd.tensor_scalar(
-                out=mean_sq[:, cols], in0=sums[:, cols], scalar1=1.0 / E, scalar2=EPS, op0=ALU.mult, op1=ALU.add
+            nc.scalar.activation(
+                out=inv_rms[:, 2 * k : 2 * k + 2], in_=sums[:, 2 * k : 2 * k + 2],
+                func=ACT.Abs_reciprocal_sqrt, scale=1.0 / E, bias=EPS,
             )
-            nc.gpsimd.tensor_tensor(out=inv_rms[:, cols], in0=mean_sq[:, cols], in1=minus_half[:], op=ALU.pow)
 
         def finish(k, banks):
             n, h = divmod(k, 2)
@@ -403,16 +405,19 @@ def tile_paired_exp_state_read_f4_kernel(
 
         pairs = 2 * GROUPS
         read_banks = {}
+        late = [(2, 1), (2, 0), (3, 0), (3, 1)]
+        for key in late[:EARLY_Q]:
+            quantize_pq(key)
+        late = late[EARLY_Q:]
         for k in range(pairs + 1):
             if k < pairs:
                 read_banks[k] = read(k)
-                square_sums(k, read_banks[k])
-                inverse_rms(k)
-                for i in range(MIX_AHEAD + 2 * k, min(MIX_AHEAD + 2 * k + 2, len(mix_list))):
-                    mix(i)
-                if 0 < k and k + 3 < pairs and pq_order[k + 3] in vector_keys:
-                    mixed[pq_order[k + 3]] = interleave(pq_rows[pq_order[k + 3]])
-                for i in range(2 if k == 0 else k + Q_AHEAD, min(k + Q_AHEAD + 1, pairs)):
-                    quantize_pq(pq_order[i])
+                square_sum(2 * k, read_banks[k][0])
+            if k >= 1:
+                inverse_rms(k - 1)
+            if k < pairs:
+                square_sum(2 * k + 1, read_banks[k][1])
             if k >= 1:
                 finish(k - 1, read_banks[k - 1])
+            if k < len(late):
+                quantize_pq(late[k])

@@ -17,6 +17,7 @@ ACT = mybir.ActivationFunctionType
 
 P = 128
 PACK = 4
+PAD = 16
 W = 512
 TOKEN_PASSES = T // W
 HALVES = F // W
@@ -24,11 +25,14 @@ GROUPS = N // W
 STEPS = HALVES * TOKEN_PASSES
 LN_LOW = 2.0 ** -63
 LN_HIGH = 2.0 ** 63
-QUERY_LAG = 3
+QUERY_LAG = 2
 FRESH_LAG = 2
-G_COLS = 384
-S_HALVES = 2
-EARLY_Q = 3
+G_COLS = 400
+G_LAST = 384
+LATE0 = 3
+S_HALVES = 1
+SKIP = 4
+EARLY = 6
 
 
 def tile_paired_exp_state_read_f4_kernel(
@@ -52,34 +56,32 @@ def tile_paired_exp_state_read_f4_kernel(
         n_tw = TOKEN_PASSES * PACK
         n_rw = HALVES * PACK
         n_w = n_tw + n_rw
-        weights = keep.tile([P, 32], BF16, name="weights")
-        gain_cols = keep.tile([P, n_rw], BF16, name="gain_cols")
-        decay_cols = keep.tile([P, n_rw], BF16, name="decay_cols")
-        nc.sync.dma_start(
-            out=weights[:, 0:n_tw].rearrange("p (c j) -> p c j", j=PACK),
-            in_=token_weight.rearrange("(c p j) -> p c j", p=P, j=PACK),
-        )
-        nc.sync.dma_start(
-            out=weights[:, n_tw:n_w].rearrange("p (g t) -> p g t", t=PACK),
-            in_=read_weight.rearrange("(g p t) -> p g t", p=P, t=PACK),
-        )
-        nc.sync.dma_start(
-            out=gain_cols[:].rearrange("p (g t) -> p g t", t=PACK),
-            in_=key_gain.rearrange("(g p t) -> p g t", p=P, t=PACK),
-        )
+        def load_quads(name, vectors):
+            counts = [v.shape[0] // W for v in vectors]
+            t = keep.tile([P, sum(counts), PAD], BF16, name=name)
+            first = 0
+            for v, count in zip(vectors, counts):
+                nc.sync.dma_start(
+                    out=t[:, first : first + count, 0:PACK], in_=v.rearrange("(c p j) -> p c j", p=P, j=PACK)
+                )
+                first = first + count
+            return t[:, :, 0:PACK]
+
+        def quads(ap):
+            return ap.rearrange("p (c j) -> p c j", j=PACK)
+
+        w_in = load_quads("weights", [token_weight, read_weight])
         keys, values, queries, states = {}, {}, {}, {}
         values[0] = load_rows("value0", block(value, 0))
         keys[0] = load_rows("key0", block(key_proj, 0))
+        gain_cols = load_quads("gain_cols", [key_gain])
         omega_rows = load_rows("omega_rows", omega)
-        queries[0] = load_rows("query0", block(query, 0))
         for c in range(1, TOKEN_PASSES):
             keys[c] = load_rows("key%d" % c, block(key_proj, c))
+            queries[c - 1] = load_rows("query%d" % (c - 1), block(query, c - 1))
             values[c] = load_rows("value%d" % c, block(value, c))
-            queries[c] = load_rows("query%d" % c, block(query, c))
-        nc.sync.dma_start(
-            out=decay_cols[:].rearrange("p (g t) -> p g t", t=PACK),
-            in_=decay.rearrange("(g p t) -> p g t", p=P, t=PACK),
-        )
+        queries[GROUPS - 1] = load_rows("query%d" % (GROUPS - 1), block(query, GROUPS - 1))
+        decay_cols = load_quads("decay_cols", [decay])
         for g in range(HALVES):
             states[g] = load_rows("state%d" % g, block(state, g))
         gain_row = keep.tile([P, E], BF16, name="gain_row")
@@ -89,12 +91,13 @@ def tile_paired_exp_state_read_f4_kernel(
         nc.vector.memset(warm[:], 1.0)
         warm_out = keep.tile([P, 1], F32, name="warm_out")
         nc.scalar.activation(out=warm_out[:], in_=warm[:], func=ACT.Ln)
+        row_length = keep.tile([P, 1], F32, name="row_length")
+        nc.vector.memset(row_length[:], float(E))
         ident_f32 = keep.tile([P, P], F32, name="ident_f32")
         make_identity(nc, ident_f32[:])
         ident_bf16 = keep.tile([P, P], BF16, name="ident_bf16")
         make_identity(nc, ident_bf16[:])
 
-        w_in = weights[:, 0:n_w]
         mag = keep.tile([P, n_w], F32, name="mag")
         half_sign = keep.tile([P, n_w], F32, name="half_sign")
         low = keep.tile([P, n_w], F32, name="low")
@@ -102,9 +105,9 @@ def tile_paired_exp_state_read_f4_kernel(
         ln_args = keep.tile([P, 2, n_w], F32, name="ln_args")
         ln_parts = keep.tile([P, 2, n_w], F32, name="ln_parts")
         ln_w = keep.tile([P, n_w], F32, name="ln_w")
-        nc.vector.scalar_tensor_tensor(out=mag[:], in0=w_in, scalar=-1.0, in1=w_in, op0=ALU.mult, op1=ALU.max)
+        nc.vector.scalar_tensor_tensor(out=quads(mag[:]), in0=w_in, scalar=-1.0, in1=w_in, op0=ALU.mult, op1=ALU.max)
         nc.vector.tensor_scalar(
-            out=half_sign[:], in0=w_in, scalar1=0.0, scalar2=0.5, op0=ALU.is_ge, op1=ALU.subtract
+            out=quads(half_sign[:]), in0=w_in, scalar1=0.0, scalar2=0.5, op0=ALU.is_ge, op1=ALU.subtract
         )
         nc.vector.tensor_scalar(out=low[:], in0=mag[:], scalar1=LN_LOW, scalar2=LN_HIGH, op0=ALU.min, op1=ALU.mult)
         nc.vector.tensor_scalar(out=high[:], in0=mag[:], scalar1=LN_HIGH, scalar2=LN_LOW, op0=ALU.max, op1=ALU.mult)
@@ -115,21 +118,14 @@ def tile_paired_exp_state_read_f4_kernel(
             out=ln_args[:, 1, :], in0=low[:], scalar=LN_LOW, in1=high[:], op0=ALU.max, op1=ALU.mult
         )
         nc.scalar.activation(out=ln_parts[:], in_=ln_args[:], func=ACT.Ln)
-        signed_gain = keep.tile([P, n_rw], BF16, name="signed_gain")
-        nc.vector.scalar_tensor_tensor(
-            out=signed_gain[:], in0=half_sign[:, n_tw:n_w], scalar=2.0, in1=gain_cols[:], op0=ALU.mult, op1=ALU.mult
-        )
         nc.vector.tensor_tensor(out=ln_w[:], in0=ln_parts[:, 0, :], in1=ln_parts[:, 1, :], op=ALU.add)
-        gain_bank = psum.tile([P, F], BF16, tag="gain", name="gain_bank")
-        for i in range(n_rw):
-            nc.tensor.transpose(
-                gain_bank[:, i * P : (i + 1) * P], signed_gain[:, i : i + 1].to_broadcast([P, P]), ident_bf16[:]
-            )
 
-        def new_grouped():
-            return work.tile([P, W * PACK], BF16, tag="grouped", name="grouped", bufs=3, align_bytes=64)
+        def new_grouped(tag="side"):
+            return work.tile([P, W * PACK], BF16, tag=tag, name=tag, bufs=2, align_bytes=64)
 
         def interleave(rows, grouped, first=0):
+            if first == W:
+                return
             nc.vector.tensor_copy(
                 out=grouped[:, first * PACK :].rearrange("p (c i j) -> p c j i", i=4, j=PACK),
                 in_=rows[:, :, first:].rearrange("p j (c i) -> p c j i", i=4),
@@ -189,7 +185,7 @@ def tile_paired_exp_state_read_f4_kernel(
 
         def key_gain_mul(s, feats):
             g = s // TOKEN_PASSES
-            grouped = new_grouped()
+            grouped = new_grouped("key_grouped")
             gains = gain_bank[:, g * W : (g + 1) * W].rearrange("p (c i) -> p c i", i=4)
             nc.vector.tensor_tensor(
                 out=grouped[:].rearrange("p (c i j) -> p c j i", i=4, j=PACK),
@@ -232,14 +228,14 @@ def tile_paired_exp_state_read_f4_kernel(
 
         pq_rows = {}
 
-        def project(i):
+        def project_slot(n, t, tag):
+            bank = psum.tile([P, W], F32, tag=tag, name="proj_bank")
+            mx(bank[:], omega_mx, t, query_mx[n], True, True)
+            return bank
+
+        def project(i, tags=("proj0", "proj1")):
             n, h = divmod(i, 2)
-            banks = []
-            for k in range(2):
-                bank = psum.tile([P, W], F32, tag="proj%d" % k, name="proj_bank")
-                mx(bank[:], omega_mx, 2 * h + k, query_mx[n], True, True)
-                banks.append(bank)
-            return banks
+            return [project_slot(n, 2 * h + k, tags[k]) for k in range(2)]
 
         def query_exps(i, banks):
             n, h = divmod(i, 2)
@@ -272,6 +268,16 @@ def tile_paired_exp_state_read_f4_kernel(
         query_grouped[0] = new_grouped()
         signed_decay = keep.tile([P, n_rw], F32, name="signed_decay")
         interleave(values[0], value_grouped)
+        signed_gain = keep.tile([P, n_rw], BF16, name="signed_gain")
+        nc.vector.scalar_tensor_tensor(
+            out=quads(signed_gain[:]), in0=quads(half_sign[:, n_tw:n_w]), scalar=2.0, in1=gain_cols, op0=ALU.mult, op1=ALU.mult
+        )
+        gain_bank = psum.tile([P, F], BF16, tag="gain", name="gain_bank")
+        for i in range(n_rw):
+            nc.tensor.transpose(
+                gain_bank[:, i * P : (i + 1) * P], signed_gain[:, i : i + 1].to_broadcast([P, P]), ident_bf16[:]
+            )
+
         value_mx[0] = quantize(value_grouped, "value", TOKEN_PASSES)
 
         pq_order = [(n, g) for n in range(GROUPS) for g in range(HALVES)]
@@ -285,139 +291,150 @@ def tile_paired_exp_state_read_f4_kernel(
         def quantize_pq(key):
             pq_mx[key] = quantize(mixed[key], "pq", 8)
 
-        first_bank = query_transposes(0, "proj0")
+        turns = {0: [0, 1], 2: [2], 3: [3], 4: [4, 5], 5: [6], 6: [7]}
+        feats = {}
         side = rows = None
         for s in range(STEPS):
-            q = s - QUERY_LAG
+            q = s - QUERY_LAG if s < SKIP else s - QUERY_LAG - 1
+            if s == SKIP:
+                q = -1
+            turn_banks = [query_transposes(i, tag) for i, tag in zip(turns.get(s, []), ("turn", "proj0"))]
             if q >= 0:
                 proj_banks = project(q)
-            if s + 1 < STEPS:
-                turn_bank = query_transposes(s + 1)
             if s >= FRESH_LAG:
                 fresh_matmuls(s - FRESH_LAG)
-            feats = key_exps(s)
             if s == 0:
-                query_copy(0, first_bank)
-            if s + 1 < STEPS:
-                query_copy(s + 1, turn_bank)
+                for i in range(2):
+                    feats[i] = key_exps(i)
+            elif s > 1:
+                feats[s] = key_exps(s)
+            for i, bank in zip(turns.get(s, []), turn_banks):
+                query_copy(i, bank)
             if q >= 0:
                 query_exps(q, proj_banks)
             update = s - FRESH_LAG == TOKEN_PASSES - 1
-            key_grouped = key_gain_mul(s, feats)
             previous_side = side
             side = new_grouped()
             if s == 0:
                 dst = side[:].rearrange("p (t m j) -> p t m j", t=PACK, j=PACK)
                 src = omega_rows[:].rearrange("p j (m t) -> p t m j", t=PACK)
+                nc.vector.tensor_copy(out=dst[:, 3], in_=src[:, 3])
                 nc.gpsimd.tensor_scalar(
                     out=dst[:, :3], in0=src[:, :3], scalar1=1.0, scalar2=1.0, op0=ALU.mult, op1=ALU.mult
                 )
-                nc.vector.tensor_copy(out=dst[:, 3], in_=src[:, 3])
-            elif update:
+            key_grouped = key_gain_mul(s, feats[s])
+            if update:
                 interleave_on_gpsimd(pq_rows[0, 1], side, W)
                 rows = state_rows(0)
-            else:
+            elif s > 0:
                 side_rows = values[s] if s < TOKEN_PASSES else {4: pq_rows[0, 0], 6: rows, 7: pq_rows.get((1, 0))}[s]
                 interleave_on_gpsimd(side_rows, side, G_COLS)
                 interleave(side_rows, side, G_COLS)
-            if s == 1:
-                omega_mx = quantize(previous_side, "omega", 1)
-            elif 1 < s <= TOKEN_PASSES:
+            if s == TOKEN_PASSES:
+                nc.vector.scalar_tensor_tensor(
+                    out=quads(signed_decay[:]), in0=quads(half_sign[:, n_tw:n_w]), scalar=2.0, in1=decay_cols,
+                    op0=ALU.mult, op1=ALU.mult,
+                )
+            if s == 0:
+                omega_mx = quantize(side, "omega", 1)
+            if s + 1 < TOKEN_PASSES:
+                sign_value(s + 1)
+            for i in turns.get(s, []):
+                if i % 2 == 1:
+                    query_mx[i // 2] = quantize(query_grouped[i // 2], "query", 2)
+            if 1 < s <= TOKEN_PASSES:
                 value_mx[s - 1] = quantize(previous_side, "value", TOKEN_PASSES)
             elif s == 5:
                 pq_mx[0, 0] = quantize(previous_side, "pq", 8)
             elif s == 6:
                 pq_mx[0, 1] = quantize(previous_side, "pq", 8)
-            elif s == 7:
-                state_mx[0] = quantize(previous_side, "state", HALVES)
-            if s % 2 == 0:
-                query_mx[s // 2] = quantize(query_grouped[s // 2], "query", 2)
-            if s + 1 < TOKEN_PASSES:
-                sign_value(s + 1)
-            if s == TOKEN_PASSES:
-                nc.vector.scalar_tensor_tensor(
-                    out=signed_decay[:], in0=half_sign[:, n_tw:n_w], scalar=2.0, in1=decay_cols[:],
-                    op0=ALU.mult, op1=ALU.mult,
-                )
             pk_mx[s] = quantize(key_grouped, "pk", 4)
 
         mixed[1, 0] = side
-        for q in range(STEPS - QUERY_LAG, STEPS):
-            proj_banks = project(q)
-            if q + QUERY_LAG - FRESH_LAG < STEPS:
-                fresh_matmuls(q + QUERY_LAG - FRESH_LAG)
-            query_exps(q, proj_banks)
-        for key in [(1, 1), (2, 0), (2, 1)]:
-            mixed[key] = new_grouped()
-        interleave(pq_rows[1, 1], mixed[1, 1])
+        proj_banks = project(STEPS - 3)
+        fresh_matmuls(STEPS - 2)
+        query_exps(STEPS - 3, proj_banks)
+        first_slot = project_slot(GROUPS - 1, 0, "turn")
+        fresh_matmuls(STEPS - 1)
+        query_exps(STEPS - 2, [first_slot, project_slot(GROUPS - 1, 1, "proj0")])
+        query_exps(STEPS - 1, project(STEPS - 1, ("proj1", "turn")))
+        state_mx[0] = quantize(previous_side, "state", HALVES)
+        mixed[2, 1] = new_grouped()
+        interleave_on_gpsimd(pq_rows[2, 1], mixed[2, 1], G_LAST)
         quantize_pq((1, 0))
-        interleave_on_gpsimd(pq_rows[2, 1], mixed[2, 1], G_COLS)
         rows = state_rows(1)
-        interleave(pq_rows[2, 1], mixed[2, 1], G_COLS)
         state_grouped = spare_grouped("state")
         interleave(rows, state_grouped)
-        quantize_pq((1, 1))
+        interleave(pq_rows[2, 1], mixed[2, 1], G_LAST)
         state_mx[1] = quantize(state_grouped, "state", HALVES)
-        interleave(pq_rows[2, 0], mixed[2, 0])
-        for i, key in enumerate([(3, 0), (3, 1)]):
-            spare_grouped(key)
-            halves = min(2, max(0, S_HALVES - 2 * i))
-            for h in range(halves):
-                interleave_half_on_scalar(pq_rows[key], mixed[key], h)
-            if halves < 2:
-                interleave(pq_rows[key], mixed[key], halves * W // 2)
+        mixed[1, 1] = new_grouped()
+        interleave(pq_rows[1, 1], mixed[1, 1])
+        interleave(pq_rows[2, 0], spare_grouped((2, 0)))
+        quantize_pq((1, 1))
+        spare_grouped((3, 0))
+        for h in range(S_HALVES):
+            interleave_half_on_scalar(pq_rows[3, 0], mixed[3, 0], h)
+        interleave(pq_rows[3, 0], mixed[3, 0], S_HALVES * W // 2)
+        quantize_pq((2, 0))
+        quantize_pq((2, 1))
+        mixed[3, 1] = new_grouped()
+        interleave_on_gpsimd(pq_rows[3, 1], mixed[3, 1], W)
+        quantize_pq((3, 0))
+        root_scale = keep.tile([P, 1], F32, name="root_scale")
+        nc.scalar.activation(out=root_scale[:], in_=row_length[:], func=ACT.Abs_reciprocal_sqrt)
 
         out_tags = ["acc0", "acc1", "acc2", "acc3", "gain", "turn", "proj0", "proj1"]
         sums = keep.tile([P, 2 * GROUPS * 2], F32, name="sums")
         inv_rms = keep.tile([P, 2 * GROUPS * 2], F32, name="inv_rms")
 
-        def read(k):
-            n, h = divmod(k, 2)
-            banks = []
-            for b in range(2):
-                bank = psum.tile([P, E], F32, tag=out_tags[(2 * k + b) % len(out_tags)], name="read_bank")
-                for g in range(HALVES):
-                    mx(bank[:], pq_mx[n, g], 2 * h + b, state_mx[g], g == 0, g == HALVES - 1)
-                banks.append(bank)
-            return banks
+        read_banks = {}
+
+        def read_pass(i, g):
+            n, b = divmod(i, PACK)
+            if g == 0:
+                read_banks[i] = psum.tile([P, E], F32, tag=out_tags[i % len(out_tags)], name="read_bank")
+            mx(read_banks[i][:], pq_mx[n, g], b, state_mx[g], g == 0, g == HALVES - 1)
 
         def square_sum(col, bank):
             squares = work.tile([P, E], BF16, tag="squares", name="squares", bufs=2)
-            nc.scalar.activation(out=squares[:], in_=bank[:], func=ACT.Square, accum_out=sums[:, col : col + 1])
+            nc.scalar.activation(out=squares[:], in_=bank[:], func=ACT.Square, scale=root_scale[:], accum_out=sums[:, col : col + 1])
 
         def inverse_rms(k):
             nc.scalar.activation(
                 out=inv_rms[:, 2 * k : 2 * k + 2], in_=sums[:, 2 * k : 2 * k + 2],
-                func=ACT.Abs_reciprocal_sqrt, scale=1.0 / E, bias=EPS,
+                func=ACT.Abs_reciprocal_sqrt, bias=EPS,
             )
 
-        def finish(k, banks):
+        def finish(k):
             n, h = divmod(k, 2)
             rows = out[n * W : (n + 1) * W, :].rearrange("(p b) e -> p b e", b=PACK)
+            result = work.tile([P, 2, E], F32, tag="result", name="result", bufs=5)
             for b in range(2):
                 col = 2 * k + b
-                result = work.tile([P, E], F32, tag="result", name="result", bufs=8)
                 nc.vector.scalar_tensor_tensor(
-                    out=result[:], in0=banks[b][:], scalar=inv_rms[:, col : col + 1], in1=gain_row[:],
+                    out=result[:, b, :], in0=read_banks[col][:], scalar=inv_rms[:, col : col + 1], in1=gain_row[:],
                     op0=ALU.mult, op1=ALU.mult,
                 )
-                nc.sync.dma_start(out=rows[:, 2 * h + b, :], in_=result[:])
+                if k == pairs - 1:
+                    nc.sync.dma_start(out=rows[:, 2 * h + b, :], in_=result[:, b, :])
+            if k < pairs - 1:
+                nc.sync.dma_start(out=rows[:, 2 * h : 2 * h + 2, :], in_=result[:])
 
         pairs = 2 * GROUPS
-        read_banks = {}
-        late = [(2, 1), (2, 0), (3, 0), (3, 1)]
-        for key in late[:EARLY_Q]:
-            quantize_pq(key)
-        late = late[EARLY_Q:]
+        for i in range(EARLY):
+            read_pass(i, 0)
         for k in range(pairs + 1):
             if k < pairs:
-                read_banks[k] = read(k)
-                square_sum(2 * k, read_banks[k][0])
+                for i in (2 * k, 2 * k + 1):
+                    if i >= EARLY:
+                        read_pass(i, 0)
+                    read_pass(i, 1)
+                square_sum(2 * k, read_banks[2 * k])
             if k >= 1:
                 inverse_rms(k - 1)
             if k < pairs:
-                square_sum(2 * k + 1, read_banks[k][1])
+                square_sum(2 * k + 1, read_banks[2 * k + 1])
             if k >= 1:
-                finish(k - 1, read_banks[k - 1])
-            if k < len(late):
-                quantize_pq(late[k])
+                finish(k - 1)
+            if k == LATE0:
+                quantize_pq((3, 1))

@@ -16,23 +16,25 @@ ALU = mybir.AluOpType
 ACT = mybir.ActivationFunctionType
 
 P = 128
-PACK = 4
-PAD = 16
-W = 512
+SLOTS = 4
+W = P * SLOTS
 TOKEN_PASSES = T // W
 HALVES = F // W
 GROUPS = N // W
 STEPS = HALVES * TOKEN_PASSES
+PAIRS = N // (2 * P)
+RUN = 4
+PAD = 16
 LN_LOW = 2.0 ** -63
 LN_HIGH = 2.0 ** 63
-QUERY_LAG = 2
+
+GPSIMD_COLUMNS = 432
+SCALAR_COLUMNS = 128
 FRESH_LAG = 2
-G_COLS = 400
-G_LAST = 384
-LATE0 = 3
-S_HALVES = 1
-SKIP = 4
-EARLY = 6
+QUERY_START = 2
+QUERY_PAUSE = 4
+EARLY_READS = 6
+GPSIMD_PAIRS = 3
 
 
 def tile_paired_exp_state_read_f4_kernel(
@@ -45,104 +47,112 @@ def tile_paired_exp_state_read_f4_kernel(
         psum = ctx.enter_context(tc.psum_pool(name="psum", bufs=1))
         ctx.enter_context(tc.manual_schedule())
 
-        def load_rows(name, rows):
-            t = keep.tile([P, PACK, W], BF16, name=name, align_bytes=64)
-            nc.sync.dma_start(out=t[:], in_=rows.rearrange("(p j) w -> p j w", j=PACK))
-            return t
+        def load_rows(name, source, block):
+            rows = keep.tile([P, SLOTS, W], BF16, name="%s%d" % (name, block), align_bytes=64)
+            source_rows = source[block * W : (block + 1) * W, :]
+            nc.sync.dma_start(out=rows[:], in_=source_rows.rearrange("(p j) w -> p j w", j=SLOTS))
+            return rows
 
-        def block(src, i):
-            return src[i * W : (i + 1) * W, :]
-
-        n_tw = TOKEN_PASSES * PACK
-        n_rw = HALVES * PACK
-        n_w = n_tw + n_rw
-        def load_quads(name, vectors):
-            counts = [v.shape[0] // W for v in vectors]
-            t = keep.tile([P, sum(counts), PAD], BF16, name=name)
+        def load_vectors(name, vectors):
+            counts = [vector.shape[0] // W for vector in vectors]
+            padded = keep.tile([P, sum(counts), PAD], BF16, name=name)
             first = 0
-            for v, count in zip(vectors, counts):
+            for vector, count in zip(vectors, counts):
                 nc.sync.dma_start(
-                    out=t[:, first : first + count, 0:PACK], in_=v.rearrange("(c p j) -> p c j", p=P, j=PACK)
+                    out=padded[:, first : first + count, 0:SLOTS],
+                    in_=vector.rearrange("(c p j) -> p c j", p=P, j=SLOTS),
                 )
                 first = first + count
-            return t[:, :, 0:PACK]
+            return padded[:, :, 0:SLOTS]
 
-        def quads(ap):
-            return ap.rearrange("p (c j) -> p c j", j=PACK)
+        def by_slot(columns):
+            return columns.rearrange("p (c j) -> p c j", j=SLOTS)
 
-        w_in = load_quads("weights", [token_weight, read_weight])
+        token_cols = TOKEN_PASSES * SLOTS
+        feature_cols = HALVES * SLOTS
+        weight_cols = token_cols + feature_cols
+        weights = load_vectors("weights", [token_weight, read_weight])
+        key_gains = load_vectors("key_gains", [key_gain])
         keys, values, queries, states = {}, {}, {}, {}
-        values[0] = load_rows("value0", block(value, 0))
-        keys[0] = load_rows("key0", block(key_proj, 0))
-        gain_cols = load_quads("gain_cols", [key_gain])
-        omega_rows = load_rows("omega_rows", omega)
+        values[0] = load_rows("value", value, 0)
+        keys[0] = load_rows("key", key_proj, 0)
+        queries[0] = load_rows("query", query, 0)
+        omega_rows = load_rows("omega", omega, 0)
         for c in range(1, TOKEN_PASSES):
-            keys[c] = load_rows("key%d" % c, block(key_proj, c))
-            queries[c - 1] = load_rows("query%d" % (c - 1), block(query, c - 1))
-            values[c] = load_rows("value%d" % c, block(value, c))
-        queries[GROUPS - 1] = load_rows("query%d" % (GROUPS - 1), block(query, GROUPS - 1))
-        decay_cols = load_quads("decay_cols", [decay])
+            keys[c] = load_rows("key", key_proj, c)
+            values[c] = load_rows("value", value, c)
+            queries[c] = load_rows("query", query, c)
+        decays = load_vectors("decays", [decay])
         for g in range(HALVES):
-            states[g] = load_rows("state%d" % g, block(state, g))
+            states[g] = load_rows("state", state, g)
         gain_row = keep.tile([P, E], BF16, name="gain_row")
         nc.sync.dma_start(out=gain_row[:], in_=norm_gain.partition_broadcast(P))
 
-        warm = keep.tile([P, 1], F32, name="warm")
-        nc.vector.memset(warm[:], 1.0)
-        warm_out = keep.tile([P, 1], F32, name="warm_out")
-        nc.scalar.activation(out=warm_out[:], in_=warm[:], func=ACT.Ln)
         row_length = keep.tile([P, 1], F32, name="row_length")
         nc.vector.memset(row_length[:], float(E))
-        ident_f32 = keep.tile([P, P], F32, name="ident_f32")
-        make_identity(nc, ident_f32[:])
-        ident_bf16 = keep.tile([P, P], BF16, name="ident_bf16")
-        make_identity(nc, ident_bf16[:])
+        identity_f32 = keep.tile([P, P], F32, name="identity_f32")
+        make_identity(nc, identity_f32[:])
+        identity_bf16 = keep.tile([P, P], BF16, name="identity_bf16")
+        make_identity(nc, identity_bf16[:])
 
-        mag = keep.tile([P, n_w], F32, name="mag")
-        half_sign = keep.tile([P, n_w], F32, name="half_sign")
-        low = keep.tile([P, n_w], F32, name="low")
-        high = keep.tile([P, n_w], F32, name="high")
-        ln_args = keep.tile([P, 2, n_w], F32, name="ln_args")
-        ln_parts = keep.tile([P, 2, n_w], F32, name="ln_parts")
-        ln_w = keep.tile([P, n_w], F32, name="ln_w")
-        nc.vector.scalar_tensor_tensor(out=quads(mag[:]), in0=w_in, scalar=-1.0, in1=w_in, op0=ALU.mult, op1=ALU.max)
-        nc.vector.tensor_scalar(
-            out=quads(half_sign[:]), in0=w_in, scalar1=0.0, scalar2=0.5, op0=ALU.is_ge, op1=ALU.subtract
+        magnitude = keep.tile([P, weight_cols], F32, name="magnitude")
+        half_sign = keep.tile([P, weight_cols], F32, name="half_sign")
+        below = keep.tile([P, weight_cols], F32, name="below")
+        above = keep.tile([P, weight_cols], F32, name="above")
+        factors = keep.tile([P, 2, weight_cols], F32, name="factors")
+        ln_factors = keep.tile([P, 2, weight_cols], F32, name="ln_factors")
+        ln_weight = keep.tile([P, weight_cols], F32, name="ln_weight")
+        nc.vector.scalar_tensor_tensor(
+            out=by_slot(magnitude[:]), in0=weights, scalar=-1.0, in1=weights, op0=ALU.mult, op1=ALU.max
         )
-        nc.vector.tensor_scalar(out=low[:], in0=mag[:], scalar1=LN_LOW, scalar2=LN_HIGH, op0=ALU.min, op1=ALU.mult)
-        nc.vector.tensor_scalar(out=high[:], in0=mag[:], scalar1=LN_HIGH, scalar2=LN_LOW, op0=ALU.max, op1=ALU.mult)
         nc.vector.tensor_scalar(
-            out=ln_args[:, 0, :], in0=mag[:], scalar1=LN_LOW, scalar2=LN_HIGH, op0=ALU.max, op1=ALU.min
+            out=by_slot(half_sign[:]), in0=weights, scalar1=0.0, scalar2=0.5, op0=ALU.is_ge, op1=ALU.subtract
+        )
+        nc.vector.tensor_scalar(
+            out=below[:], in0=magnitude[:], scalar1=LN_LOW, scalar2=LN_HIGH, op0=ALU.min, op1=ALU.mult
+        )
+        nc.vector.tensor_scalar(
+            out=above[:], in0=magnitude[:], scalar1=LN_HIGH, scalar2=LN_LOW, op0=ALU.max, op1=ALU.mult
+        )
+        nc.vector.tensor_scalar(
+            out=factors[:, 0, :], in0=magnitude[:], scalar1=LN_LOW, scalar2=LN_HIGH, op0=ALU.max, op1=ALU.min
         )
         nc.vector.scalar_tensor_tensor(
-            out=ln_args[:, 1, :], in0=low[:], scalar=LN_LOW, in1=high[:], op0=ALU.max, op1=ALU.mult
+            out=factors[:, 1, :], in0=below[:], scalar=LN_LOW, in1=above[:], op0=ALU.max, op1=ALU.mult
         )
-        nc.scalar.activation(out=ln_parts[:], in_=ln_args[:], func=ACT.Ln)
-        nc.vector.tensor_tensor(out=ln_w[:], in0=ln_parts[:, 0, :], in1=ln_parts[:, 1, :], op=ALU.add)
+        nc.scalar.activation(out=ln_factors[:], in_=factors[:], func=ACT.Ln)
+        nc.vector.tensor_tensor(out=ln_weight[:], in0=ln_factors[:, 0, :], in1=ln_factors[:, 1, :], op=ALU.add)
 
-        def new_grouped(tag="side"):
-            return work.tile([P, W * PACK], BF16, tag=tag, name=tag, bufs=2, align_bytes=64)
+        def times_read_sign(name, columns, dtype):
+            signed = keep.tile([P, feature_cols], dtype, name=name)
+            nc.vector.scalar_tensor_tensor(
+                out=by_slot(signed[:]), in0=by_slot(half_sign[:, token_cols:weight_cols]), scalar=2.0,
+                in1=columns, op0=ALU.mult, op1=ALU.mult,
+            )
+            return signed
+
+        def new_grouped(tag, bufs):
+            return work.tile([P, W * SLOTS], BF16, tag=tag, name=tag, bufs=bufs, align_bytes=64)
+
+        def new_side():
+            return new_grouped("side", 1)
+
+        def in_runs(rows, grouped, first, last):
+            source = rows[:, :, first:last].rearrange("p j (c i) -> p c j i", i=RUN)
+            target = grouped[:, first * SLOTS : last * SLOTS].rearrange("p (c i j) -> p c j i", i=RUN, j=SLOTS)
+            return source, target
 
         def interleave(rows, grouped, first=0):
-            if first == W:
-                return
-            nc.vector.tensor_copy(
-                out=grouped[:, first * PACK :].rearrange("p (c i j) -> p c j i", i=4, j=PACK),
-                in_=rows[:, :, first:].rearrange("p j (c i) -> p c j i", i=4),
-            )
+            source, target = in_runs(rows, grouped, first, W)
+            nc.vector.tensor_copy(out=target, in_=source)
 
-        def interleave_on_gpsimd(rows, grouped, count):
-            nc.gpsimd.tensor_scalar(
-                out=grouped[:, : count * PACK].rearrange("p (w j) -> p w j", j=PACK),
-                in0=rows[:, :, :count].rearrange("p j w -> p w j"),
-                scalar1=1.0, scalar2=1.0, op0=ALU.mult, op1=ALU.mult,
-            )
+        def move_on_gpsimd(target, source):
+            nc.gpsimd.tensor_scalar(out=target, in0=source, scalar1=1.0, scalar2=1.0, op0=ALU.mult, op1=ALU.mult)
 
-        def interleave_half_on_scalar(rows, grouped, h):
-            half = W // 2
-            nc.scalar.copy(
-                out=grouped[:, h * half * PACK : (h + 1) * half * PACK].rearrange("p (c i j) -> p c j i", i=4, j=PACK),
-                in_=rows[:, :, h * half : (h + 1) * half].rearrange("p j (c i) -> p c j i", i=4),
+        def interleave_on_gpsimd(rows, grouped, last):
+            move_on_gpsimd(
+                grouped[:, : last * SLOTS].rearrange("p (w j) -> p w j", j=SLOTS),
+                rows[:, :, :last].rearrange("p j w -> p w j"),
             )
 
         def quantize(grouped, tag, bufs):
@@ -151,290 +161,283 @@ def tile_paired_exp_state_read_f4_kernel(
             nc.vector.quantize_mx(out=codes[:].bitcast(FP8X4), scales=scales[:], in_=grouped[:])
             return codes, scales
 
-        def mx(acc, stationary, col, moving, start, stop):
-            cols = slice(col * P, (col + 1) * P)
+        def matmul_pass(bank, stationary, tile_index, moving, start, stop):
+            columns = slice(tile_index * P, (tile_index + 1) * P)
             nc.tensor.matmul_mx(
-                out=acc,
-                lhsT=stationary[0][:, cols].bitcast(FP8X4),
-                lhsT_scale=stationary[1][:, cols],
+                out=bank[:],
+                lhsT=stationary[0][:, columns].bitcast(FP8X4),
+                lhsT_scale=stationary[1][:, columns],
                 rhs=moving[0][:].bitcast(FP8X4),
                 rhs_scale=moving[1][:],
                 start=start,
                 stop=stop,
             )
 
+        pk_mx, value_mx, query_mx, pq_mx, state_mx = {}, {}, {}, {}, {}
+        fresh_banks, query_grouped, pq_rows, pq_grouped = {}, {}, {}, {}
+
         def sign_value(c):
-            for j in range(PACK):
-                col = c * PACK + j
+            for j in range(SLOTS):
+                col = c * SLOTS + j
                 nc.vector.tensor_scalar(
                     out=values[c][:, j, :], in0=values[c][:, j, :], scalar1=half_sign[:, col : col + 1],
                     scalar2=2.0, op0=ALU.mult, op1=ALU.mult,
                 )
 
-        def key_exps(s):
-            g, c = divmod(s, TOKEN_PASSES)
-            feats = work.tile([P, PACK, W], F32, tag="key_feats", name="key_feats", bufs=3)
-            for j in range(PACK):
-                col = c * PACK + j
-                nc.scalar.activation(
-                    out=feats[:, j, :].rearrange("p (t m) -> p t m", t=PACK),
-                    in_=keys[c][:, j, :].rearrange("p (m t) -> p t m", t=PACK),
-                    func=ACT.Exp, scale=1.0 - 2.0 * g, bias=ln_w[:, col : col + 1],
-                )
-            return feats
+        def column_pieces(step):
+            width = W // 2 if step == 0 else W
+            return [(first, first + width) for first in range(0, W, width)]
 
-        def key_gain_mul(s, feats):
-            g = s // TOKEN_PASSES
-            grouped = new_grouped("key_grouped")
-            gains = gain_bank[:, g * W : (g + 1) * W].rearrange("p (c i) -> p c i", i=4)
-            nc.vector.tensor_tensor(
-                out=grouped[:].rearrange("p (c i j) -> p c j i", i=4, j=PACK),
-                in0=feats[:].rearrange("p j (c i) -> p c j i", i=4),
-                in1=gains.unsqueeze(2).to_broadcast([P, W // 4, PACK, 4]),
-                op=ALU.mult,
-            )
+        def key_exps(step):
+            g, c = divmod(step, TOKEN_PASSES)
+            features = work.tile([P, SLOTS, W], F32, tag="key_features", name="key_features", bufs=3)
+            for first, last in column_pieces(step):
+                tiles = slice(first // P, last // P)
+                for j in range(SLOTS):
+                    col = c * SLOTS + j
+                    nc.scalar.activation(
+                        out=features[:, j, :].rearrange("p (t m) -> p t m", t=SLOTS)[:, tiles],
+                        in_=keys[c][:, j, :].rearrange("p (m t) -> p t m", t=SLOTS)[:, tiles],
+                        func=ACT.Exp, scale=1.0 - 2.0 * g, bias=ln_weight[:, col : col + 1],
+                    )
+            return features
+
+        def times_key_gain(step, features):
+            g = step // TOKEN_PASSES
+            grouped = new_grouped("pk_grouped", 2)
+            for first, last in column_pieces(step):
+                source, target = in_runs(features, grouped, first, last)
+                gains = gain_bank[:, g * W + first : g * W + last].rearrange("p (c i) -> p c i", i=RUN)
+                gains = gains.unsqueeze(2).to_broadcast([P, (last - first) // RUN, SLOTS, RUN])
+                nc.vector.tensor_tensor(out=target, in0=source, in1=gains, op=ALU.mult)
             return grouped
 
-        fresh = {}
-
-        def fresh_matmuls(s):
-            g, c = divmod(s, TOKEN_PASSES)
-            for t in range(PACK):
+        def fresh_passes(step):
+            g, c = divmod(step, TOKEN_PASSES)
+            for t in range(SLOTS):
                 if c == 0:
-                    fresh[g, t] = psum.tile([P, E], F32, tag="acc%d" % t, name="fresh")
-                mx(fresh[g, t][:], pk_mx[s], t, value_mx[c], c == 0, c == TOKEN_PASSES - 1)
+                    fresh_banks[g, t] = psum.tile([P, E], F32, tag="sum%d" % t, name="fresh_bank")
+                matmul_pass(fresh_banks[g, t], pk_mx[step], t, value_mx[c], c == 0, c == TOKEN_PASSES - 1)
 
-        query_grouped = {}
-
-        def query_transposes(i, tag="turn"):
-            n, h = divmod(i, 2)
-            if n not in query_grouped:
-                query_grouped[n] = work.tile(
-                    [P, W * PACK], BF16, tag="query_grouped", name="query_grouped", bufs=2, align_bytes=64
+        def updated_state_rows(g):
+            rows = work.tile([P, SLOTS, E], BF16, tag="state_rows", name="state_rows", bufs=HALVES)
+            for t in range(SLOTS):
+                col = g * SLOTS + t
+                nc.vector.scalar_tensor_tensor(
+                    out=rows[:, t, :], in0=states[g][:, t, :], scalar=signed_decay[:, col : col + 1],
+                    in1=fresh_banks[g, t][:], op0=ALU.mult, op1=ALU.add,
                 )
+            return rows
+
+        def transpose_queries(index, tag):
+            n, h = divmod(index, 2)
+            if h == 0:
+                query_grouped[n] = new_grouped("query_grouped", 2)
             bank = psum.tile([P, 2, 2, P], F32, tag=tag, name="turn_bank")
             for b in range(2):
                 words = queries[n][:, 2 * h + b, :].bitcast(F32)
                 for u in range(2):
-                    nc.tensor.transpose(bank[:, b, u, :], words[:, u : 2 * P : 2], ident_f32[:])
+                    nc.tensor.transpose(bank[:, b, u, :], words[:, u : 2 * P : 2], identity_f32[:])
             return bank
 
-        def query_copy(i, bank):
-            n, h = divmod(i, 2)
-            dst = query_grouped[n][:, h * 2 * W : (h + 1) * 2 * W].bitcast(F32)
+        def copy_queries(index, bank):
+            n, h = divmod(index, 2)
+            words = query_grouped[n][:, h * 2 * W : (h + 1) * 2 * W].bitcast(F32)
             nc.scalar.copy(
-                out=dst.rearrange("p (b r u) -> p b r u", b=2, u=2), in_=bank[:].rearrange("p b u r -> p b r u")
+                out=words.rearrange("p (b r u) -> p b r u", b=2, u=2), in_=bank[:].rearrange("p b u r -> p b r u")
             )
 
-        pq_rows = {}
-
         def project_slot(n, t, tag):
-            bank = psum.tile([P, W], F32, tag=tag, name="proj_bank")
-            mx(bank[:], omega_mx, t, query_mx[n], True, True)
+            bank = psum.tile([P, W], F32, tag=tag, name="projection_bank")
+            matmul_pass(bank, omega_mx, t, query_mx[n], True, True)
             return bank
 
-        def project(i, tags=("proj0", "proj1")):
-            n, h = divmod(i, 2)
+        def project(part, tags=("project0", "project1")):
+            n, h = divmod(part, 2)
             return [project_slot(n, 2 * h + k, tags[k]) for k in range(2)]
 
-        def query_exps(i, banks):
-            n, h = divmod(i, 2)
+        def query_exps(part, banks):
+            n, h = divmod(part, 2)
             if h == 0:
                 for g in range(HALVES):
-                    pq_rows[n, g] = work.tile([P, PACK, W], BF16, tag="pq_rows", name="pq_rows", bufs=8)
+                    pq_rows[n, g] = work.tile([P, SLOTS, W], BF16, tag="pq_rows", name="pq_rows", bufs=GROUPS * HALVES)
             for k in range(2):
                 t = 2 * h + k
                 for g in range(HALVES):
-                    col = n_tw + g * PACK + t
+                    col = token_cols + g * SLOTS + t
                     nc.scalar.activation(
                         out=pq_rows[n, g][:, t, :], in_=banks[k][:], func=ACT.Exp,
-                        scale=1.0 - 2.0 * g, bias=ln_w[:, col : col + 1],
+                        scale=1.0 - 2.0 * g, bias=ln_weight[:, col : col + 1],
                     )
 
-        def state_rows(g):
-            rows = work.tile([P, PACK, E], BF16, tag="state_rows", name="state_rows", bufs=2)
-            for t in range(PACK):
-                col = g * PACK + t
-                nc.vector.scalar_tensor_tensor(
-                    out=rows[:, t, :], in0=states[g][:, t, :], scalar=signed_decay[:, col : col + 1],
-                    in1=fresh[g, t][:], op0=ALU.mult, op1=ALU.add,
-                )
-            return rows
-
-        pk_mx, value_mx, query_mx, pq_mx, state_mx = {}, {}, {}, {}, {}
+        def quantize_pq(n, g, grouped):
+            pq_mx[n, g] = quantize(grouped, "pq", GROUPS * HALVES)
 
         sign_value(0)
-        value_grouped = new_grouped()
-        query_grouped[0] = new_grouped()
-        signed_decay = keep.tile([P, n_rw], F32, name="signed_decay")
+        value_grouped = new_side()
+        signed_gain = times_read_sign("signed_gain", key_gains, BF16)
         interleave(values[0], value_grouped)
-        signed_gain = keep.tile([P, n_rw], BF16, name="signed_gain")
-        nc.vector.scalar_tensor_tensor(
-            out=quads(signed_gain[:]), in0=quads(half_sign[:, n_tw:n_w]), scalar=2.0, in1=gain_cols, op0=ALU.mult, op1=ALU.mult
-        )
         gain_bank = psum.tile([P, F], BF16, tag="gain", name="gain_bank")
-        for i in range(n_rw):
+        for col in range(feature_cols):
             nc.tensor.transpose(
-                gain_bank[:, i * P : (i + 1) * P], signed_gain[:, i : i + 1].to_broadcast([P, P]), ident_bf16[:]
+                gain_bank[:, col * P : (col + 1) * P],
+                signed_gain[:, col : col + 1].to_broadcast([P, P]),
+                identity_bf16[:],
             )
-
         value_mx[0] = quantize(value_grouped, "value", TOKEN_PASSES)
 
-        pq_order = [(n, g) for n in range(GROUPS) for g in range(HALVES)]
-        spare_tags = ["value%d" % c for c in range(TOKEN_PASSES)] + ["query%d" % n for n in range(GROUPS)]
-        mixed = {}
+        update_step = TOKEN_PASSES - 1 + FRESH_LAG
+        next_turn = next_part = 0
+        for step in range(STEPS):
+            projects = step >= QUERY_START and step != QUERY_PAUSE
+            turn_count = 0 if step == 1 else 1 if projects else 2
+            turns = range(next_turn, min(next_turn + turn_count, 2 * GROUPS))
+            next_turn = turns.stop
+            turn_banks = [transpose_queries(index, tag) for index, tag in zip(turns, ("turn", "project0"))]
+            if projects:
+                projection_banks = project(next_part)
+            if step >= FRESH_LAG:
+                fresh_passes(step - FRESH_LAG)
 
-        def spare_grouped(key):
-            mixed[key] = keep.tile([P, W * PACK], BF16, tag=spare_tags.pop(0), name="mixed", align_bytes=64)
-            return mixed[key]
+            features = key_exps(step)
+            for index, bank in zip(turns, turn_banks):
+                copy_queries(index, bank)
+            if projects:
+                query_exps(next_part, projection_banks)
+                next_part = next_part + 1
 
-        def quantize_pq(key):
-            pq_mx[key] = quantize(mixed[key], "pq", 8)
-
-        turns = {0: [0, 1], 2: [2], 3: [3], 4: [4, 5], 5: [6], 6: [7]}
-        feats = {}
-        side = rows = None
-        for s in range(STEPS):
-            q = s - QUERY_LAG if s < SKIP else s - QUERY_LAG - 1
-            if s == SKIP:
-                q = -1
-            turn_banks = [query_transposes(i, tag) for i, tag in zip(turns.get(s, []), ("turn", "proj0"))]
-            if q >= 0:
-                proj_banks = project(q)
-            if s >= FRESH_LAG:
-                fresh_matmuls(s - FRESH_LAG)
-            if s == 0:
-                for i in range(2):
-                    feats[i] = key_exps(i)
-            elif s > 1:
-                feats[s] = key_exps(s)
-            for i, bank in zip(turns.get(s, []), turn_banks):
-                query_copy(i, bank)
-            if q >= 0:
-                query_exps(q, proj_banks)
-            update = s - FRESH_LAG == TOKEN_PASSES - 1
-            previous_side = side
-            side = new_grouped()
-            if s == 0:
-                dst = side[:].rearrange("p (t m j) -> p t m j", t=PACK, j=PACK)
-                src = omega_rows[:].rearrange("p j (m t) -> p t m j", t=PACK)
-                nc.vector.tensor_copy(out=dst[:, 3], in_=src[:, 3])
-                nc.gpsimd.tensor_scalar(
-                    out=dst[:, :3], in0=src[:, :3], scalar1=1.0, scalar2=1.0, op0=ALU.mult, op1=ALU.mult
-                )
-            key_grouped = key_gain_mul(s, feats[s])
-            if update:
+            side = new_side()
+            pk_grouped = times_key_gain(step, features)
+            if step == 0:
+                target = side[:].rearrange("p (t m j) -> p t m j", t=SLOTS, j=SLOTS)
+                source = omega_rows[:].rearrange("p j (m t) -> p t m j", t=SLOTS)
+                move_on_gpsimd(target[:, : SLOTS - 1], source[:, : SLOTS - 1])
+                nc.vector.tensor_copy(out=target[:, SLOTS - 1], in_=source[:, SLOTS - 1])
+            elif step == update_step:
                 interleave_on_gpsimd(pq_rows[0, 1], side, W)
-                rows = state_rows(0)
-            elif s > 0:
-                side_rows = values[s] if s < TOKEN_PASSES else {4: pq_rows[0, 0], 6: rows, 7: pq_rows.get((1, 0))}[s]
-                interleave_on_gpsimd(side_rows, side, G_COLS)
-                interleave(side_rows, side, G_COLS)
-            if s == TOKEN_PASSES:
-                nc.vector.scalar_tensor_tensor(
-                    out=quads(signed_decay[:]), in0=quads(half_sign[:, n_tw:n_w]), scalar=2.0, in1=decay_cols,
-                    op0=ALU.mult, op1=ALU.mult,
-                )
-            if s == 0:
+                state_rows = updated_state_rows(0)
+            else:
+                if step < TOKEN_PASSES:
+                    side_rows = values[step]
+                elif step < update_step:
+                    side_rows = pq_rows[0, 0]
+                elif step == update_step + 1:
+                    side_rows = state_rows
+                else:
+                    side_rows = pq_rows[1, 0]
+                interleave_on_gpsimd(side_rows, side, GPSIMD_COLUMNS)
+                interleave(side_rows, side, GPSIMD_COLUMNS)
+            if step == update_step - 1:
+                signed_decay = times_read_sign("signed_decay", decays, F32)
+            if step + 1 < TOKEN_PASSES:
+                sign_value(step + 1)
+            for index in turns:
+                if index % 2 == 1:
+                    query_mx[index // 2] = quantize(query_grouped[index // 2], "query", 2)
+            if step == 0:
                 omega_mx = quantize(side, "omega", 1)
-            if s + 1 < TOKEN_PASSES:
-                sign_value(s + 1)
-            for i in turns.get(s, []):
-                if i % 2 == 1:
-                    query_mx[i // 2] = quantize(query_grouped[i // 2], "query", 2)
-            if 1 < s <= TOKEN_PASSES:
-                value_mx[s - 1] = quantize(previous_side, "value", TOKEN_PASSES)
-            elif s == 5:
-                pq_mx[0, 0] = quantize(previous_side, "pq", 8)
-            elif s == 6:
-                pq_mx[0, 1] = quantize(previous_side, "pq", 8)
-            pk_mx[s] = quantize(key_grouped, "pk", 4)
+            elif step < TOKEN_PASSES:
+                value_mx[step] = quantize(side, "value", TOKEN_PASSES)
+            elif step <= update_step:
+                quantize_pq(0, step - TOKEN_PASSES, side)
+            elif step == update_step + 1:
+                state_mx[0] = quantize(side, "state", HALVES)
+            pk_mx[step] = quantize(pk_grouped, "pk", FRESH_LAG + 2)
 
-        mixed[1, 0] = side
-        proj_banks = project(STEPS - 3)
-        fresh_matmuls(STEPS - 2)
-        query_exps(STEPS - 3, proj_banks)
-        first_slot = project_slot(GROUPS - 1, 0, "turn")
-        fresh_matmuls(STEPS - 1)
-        query_exps(STEPS - 2, [first_slot, project_slot(GROUPS - 1, 1, "proj0")])
-        query_exps(STEPS - 1, project(STEPS - 1, ("proj1", "turn")))
-        state_mx[0] = quantize(previous_side, "state", HALVES)
-        mixed[2, 1] = new_grouped()
-        interleave_on_gpsimd(pq_rows[2, 1], mixed[2, 1], G_LAST)
-        quantize_pq((1, 0))
-        rows = state_rows(1)
-        state_grouped = spare_grouped("state")
-        interleave(rows, state_grouped)
-        interleave(pq_rows[2, 1], mixed[2, 1], G_LAST)
+        last_group = GROUPS - 1
+        projection_banks = [project_slot(last_group - 1, 2, "project0")]
+        fresh_passes(STEPS - 2)
+        projection_banks.append(project_slot(last_group - 1, 3, "project1"))
+        first_slot_bank = project_slot(last_group, 0, "turn")
+        query_exps(next_part, projection_banks)
+        fresh_passes(STEPS - 1)
+        query_exps(2 * last_group, [first_slot_bank, project_slot(last_group, 1, "project0")])
+        query_exps(2 * last_group + 1, project(2 * last_group + 1, ("project1", "turn")))
+
+        def reuse_value_tile(c):
+            return keep.tile([P, W * SLOTS], BF16, tag="value%d" % c, name="late_grouped", align_bytes=64)
+
+        quantize_pq(1, 0, side)
+        pq_grouped[2, 1] = new_side()
+        interleave_on_gpsimd(pq_rows[2, 1], pq_grouped[2, 1], GPSIMD_COLUMNS)
+        pq_grouped[1, 1] = reuse_value_tile(3)
+        interleave(pq_rows[1, 1], pq_grouped[1, 1])
+        state_rows = updated_state_rows(1)
+        state_grouped = reuse_value_tile(0)
+        interleave(state_rows, state_grouped)
+        interleave(pq_rows[2, 1], pq_grouped[2, 1], GPSIMD_COLUMNS)
         state_mx[1] = quantize(state_grouped, "state", HALVES)
-        mixed[1, 1] = new_grouped()
-        interleave(pq_rows[1, 1], mixed[1, 1])
-        interleave(pq_rows[2, 0], spare_grouped((2, 0)))
-        quantize_pq((1, 1))
-        spare_grouped((3, 0))
-        for h in range(S_HALVES):
-            interleave_half_on_scalar(pq_rows[3, 0], mixed[3, 0], h)
-        interleave(pq_rows[3, 0], mixed[3, 0], S_HALVES * W // 2)
-        quantize_pq((2, 0))
-        quantize_pq((2, 1))
-        mixed[3, 1] = new_grouped()
-        interleave_on_gpsimd(pq_rows[3, 1], mixed[3, 1], W)
-        quantize_pq((3, 0))
+
+        pq_grouped[2, 0] = reuse_value_tile(1)
+        interleave(pq_rows[2, 0], pq_grouped[2, 0])
+        quantize_pq(1, 1, pq_grouped[1, 1])
+        pq_grouped[3, 0] = reuse_value_tile(2)
+        source, target = in_runs(pq_rows[3, 0], pq_grouped[3, 0], 0, SCALAR_COLUMNS)
+        nc.scalar.copy(out=target, in_=source)
+        interleave(pq_rows[3, 0], pq_grouped[3, 0], SCALAR_COLUMNS)
+        quantize_pq(2, 0, pq_grouped[2, 0])
+        quantize_pq(2, 1, pq_grouped[2, 1])
+        pq_grouped[3, 1] = new_side()
+        interleave_on_gpsimd(pq_rows[3, 1], pq_grouped[3, 1], W)
+        quantize_pq(3, 0, pq_grouped[3, 0])
+
         root_scale = keep.tile([P, 1], F32, name="root_scale")
         nc.scalar.activation(out=root_scale[:], in_=row_length[:], func=ACT.Abs_reciprocal_sqrt)
-
-        out_tags = ["acc0", "acc1", "acc2", "acc3", "gain", "turn", "proj0", "proj1"]
-        sums = keep.tile([P, 2 * GROUPS * 2], F32, name="sums")
-        inv_rms = keep.tile([P, 2 * GROUPS * 2], F32, name="inv_rms")
-
+        bank_tags = ["sum0", "sum1", "sum2", "sum3", "gain", "turn", "project0", "project1"]
+        mean_square = keep.tile([P, 2 * PAIRS], F32, name="mean_square")
+        inverse_rms = keep.tile([P, 2 * PAIRS], F32, name="inverse_rms")
         read_banks = {}
 
-        def read_pass(i, g):
-            n, b = divmod(i, PACK)
+        def read_pass(tile_index, g):
+            n, b = divmod(tile_index, SLOTS)
             if g == 0:
-                read_banks[i] = psum.tile([P, E], F32, tag=out_tags[i % len(out_tags)], name="read_bank")
-            mx(read_banks[i][:], pq_mx[n, g], b, state_mx[g], g == 0, g == HALVES - 1)
+                tag = bank_tags[tile_index % len(bank_tags)]
+                read_banks[tile_index] = psum.tile([P, E], F32, tag=tag, name="read_bank")
+            matmul_pass(read_banks[tile_index], pq_mx[n, g], b, state_mx[g], g == 0, g == HALVES - 1)
 
-        def square_sum(col, bank):
+        def sum_squares(tile_index):
             squares = work.tile([P, E], BF16, tag="squares", name="squares", bufs=2)
-            nc.scalar.activation(out=squares[:], in_=bank[:], func=ACT.Square, scale=root_scale[:], accum_out=sums[:, col : col + 1])
-
-        def inverse_rms(k):
             nc.scalar.activation(
-                out=inv_rms[:, 2 * k : 2 * k + 2], in_=sums[:, 2 * k : 2 * k + 2],
-                func=ACT.Abs_reciprocal_sqrt, bias=EPS,
+                out=squares[:], in_=read_banks[tile_index][:], func=ACT.Square, scale=root_scale[:],
+                accum_out=mean_square[:, tile_index : tile_index + 1],
             )
 
-        def finish(k):
-            n, h = divmod(k, 2)
-            rows = out[n * W : (n + 1) * W, :].rearrange("(p b) e -> p b e", b=PACK)
+        def invert_rms(pair):
+            columns = slice(2 * pair, 2 * pair + 2)
+            nc.scalar.activation(
+                out=inverse_rms[:, columns], in_=mean_square[:, columns], func=ACT.Abs_reciprocal_sqrt, bias=EPS
+            )
+
+        def finish(pair):
+            n, h = divmod(pair, 2)
+            rows = out[n * W : (n + 1) * W, :].rearrange("(r b) e -> r b e", b=SLOTS)
             result = work.tile([P, 2, E], F32, tag="result", name="result", bufs=5)
             for b in range(2):
-                col = 2 * k + b
+                tile_index = 2 * pair + b
                 nc.vector.scalar_tensor_tensor(
-                    out=result[:, b, :], in0=read_banks[col][:], scalar=inv_rms[:, col : col + 1], in1=gain_row[:],
+                    out=result[:, b, :], in0=read_banks[tile_index][:],
+                    scalar=inverse_rms[:, tile_index : tile_index + 1], in1=gain_row[:],
                     op0=ALU.mult, op1=ALU.mult,
                 )
-                if k == pairs - 1:
+                if pair == PAIRS - 1:
                     nc.sync.dma_start(out=rows[:, 2 * h + b, :], in_=result[:, b, :])
-            if k < pairs - 1:
+            if pair < PAIRS - 1:
                 nc.sync.dma_start(out=rows[:, 2 * h : 2 * h + 2, :], in_=result[:])
 
-        pairs = 2 * GROUPS
-        for i in range(EARLY):
-            read_pass(i, 0)
-        for k in range(pairs + 1):
-            if k < pairs:
-                for i in (2 * k, 2 * k + 1):
-                    if i >= EARLY:
-                        read_pass(i, 0)
-                    read_pass(i, 1)
-                square_sum(2 * k, read_banks[2 * k])
-            if k >= 1:
-                inverse_rms(k - 1)
-            if k < pairs:
-                square_sum(2 * k + 1, read_banks[2 * k + 1])
-            if k >= 1:
-                finish(k - 1)
-            if k == LATE0:
-                quantize_pq((3, 1))
+        for tile_index in range(EARLY_READS):
+            read_pass(tile_index, 0)
+        for pair in range(PAIRS + 1):
+            if pair < PAIRS:
+                for tile_index in (2 * pair, 2 * pair + 1):
+                    if tile_index >= EARLY_READS:
+                        read_pass(tile_index, 0)
+                    read_pass(tile_index, 1)
+                sum_squares(2 * pair)
+            if pair >= 1:
+                invert_rms(pair - 1)
+            if pair < PAIRS:
+                sum_squares(2 * pair + 1)
+            if pair >= 1:
+                finish(pair - 1)
+            if pair == GPSIMD_PAIRS:
+                quantize_pq(3, 1, pq_grouped[3, 1])

@@ -411,6 +411,7 @@ def tile_paired_exp_state_read_f4_kernel(
         def finish(pair):
             n, h = divmod(pair, 2)
             rows = out[n * W : (n + 1) * W, :].rearrange("(r b) e -> r b e", b=SLOTS)
+            by_tile = pair in (0, PAIRS - 1)
             result = work.tile([P, 2, E], F32, tag="result", name="result", bufs=5)
             for b in range(2):
                 tile_index = 2 * pair + b
@@ -419,9 +420,9 @@ def tile_paired_exp_state_read_f4_kernel(
                     scalar=inverse_rms[:, tile_index : tile_index + 1], in1=gain_row[:],
                     op0=ALU.mult, op1=ALU.mult,
                 )
-                if pair == PAIRS - 1:
+                if by_tile:
                     nc.sync.dma_start(out=rows[:, 2 * h + b, :], in_=result[:, b, :])
-            if pair < PAIRS - 1:
+            if not by_tile:
                 nc.sync.dma_start(out=rows[:, 2 * h : 2 * h + 2, :], in_=result[:])
 
         for tile_index in range(EARLY_READS):

from contextlib import ExitStack

import concourse.mybir as mybir
from concourse.masks import make_identity

T, N, D, R, F, E = 2048, 2048, 512, 512, 1024, 512
EPS = 1e-5
FLOPS = 2 * T * F * E + 2 * N * D * R + 2 * N * F * E

F32 = mybir.dt.float32
BF16 = mybir.dt.bfloat16
U32 = mybir.dt.uint32
U8 = mybir.dt.uint8
FP8X4 = mybir.dt.float8_e4m3fn_x4
ALU = mybir.AluOpType
ACT = mybir.ActivationFunctionType

P = 128
SLOTS = 4
W = P * SLOTS
TOKEN_PASSES = T // W
HALVES = F // W
GROUPS = N // W
STEPS = HALVES * TOKEN_PASSES
PAIRS = N // (2 * P)
RUN = 4
PAD = 16
LN_LOW = 2.0 ** -63
LN_HIGH = 2.0 ** 63

GPSIMD_COLUMNS = 432
SCALAR_COLUMNS = 128
FRESH_LAG = 2
QUERY_START = 2
QUERY_PAUSE = 4
EARLY_READS = 6
GPSIMD_PAIRS = 3


def tile_paired_exp_state_read_f4_kernel(
    tc, key_proj, token_weight, key_gain, value, state, decay, query, omega, read_weight, norm_gain, out
):
    nc = tc.nc
    with ExitStack() as ctx:
        keep = ctx.enter_context(tc.tile_pool(name="keep", bufs=1))
        work = ctx.enter_context(tc.tile_pool(name="work", bufs=1))
        psum = ctx.enter_context(tc.psum_pool(name="psum", bufs=1))
        ctx.enter_context(tc.manual_schedule())

        def load_rows(name, source, block):
            rows = keep.tile([P, SLOTS, W], BF16, name="%s%d" % (name, block), align_bytes=64)
            source_rows = source[block * W : (block + 1) * W, :]
            nc.sync.dma_start(out=rows[:], in_=source_rows.rearrange("(p j) w -> p j w", j=SLOTS))
            return rows

        def load_vectors(name, vectors):
            counts = [vector.shape[0] // W for vector in vectors]
            padded = keep.tile([P, sum(counts), PAD], BF16, name=name)
            first = 0
            for vector, count in zip(vectors, counts):
                nc.sync.dma_start(
                    out=padded[:, first : first + count, 0:SLOTS],
                    in_=vector.rearrange("(c p j) -> p c j", p=P, j=SLOTS),
                )
                first = first + count
            return padded[:, :, 0:SLOTS]

        def by_slot(columns):
            return columns.rearrange("p (c j) -> p c j", j=SLOTS)

        token_cols = TOKEN_PASSES * SLOTS
        feature_cols = HALVES * SLOTS
        weight_cols = token_cols + feature_cols
        weights = load_vectors("weights", [token_weight, read_weight])
        key_gains = load_vectors("key_gains", [key_gain])
        keys, values, queries, states = {}, {}, {}, {}
        values[0] = load_rows("value", value, 0)
        keys[0] = load_rows("key", key_proj, 0)
        queries[0] = load_rows("query", query, 0)
        omega_rows = load_rows("omega", omega, 0)
        for c in range(1, TOKEN_PASSES):
            keys[c] = load_rows("key", key_proj, c)
            values[c] = load_rows("value", value, c)
            queries[c] = load_rows("query", query, c)
        decays = load_vectors("decays", [decay])
        for g in range(HALVES):
            states[g] = load_rows("state", state, g)
        gain_row = keep.tile([P, E], BF16, name="gain_row")
        nc.sync.dma_start(out=gain_row[:], in_=norm_gain.partition_broadcast(P))

        row_length = keep.tile([P, 1], F32, name="row_length")
        nc.vector.memset(row_length[:], float(E))
        identity_f32 = keep.tile([P, P], F32, name="identity_f32")
        make_identity(nc, identity_f32[:])
        identity_bf16 = keep.tile([P, P], BF16, name="identity_bf16")
        make_identity(nc, identity_bf16[:])

        magnitude = keep.tile([P, weight_cols], F32, name="magnitude")
        half_sign = keep.tile([P, weight_cols], F32, name="half_sign")
        below = keep.tile([P, weight_cols], F32, name="below")
        above = keep.tile([P, weight_cols], F32, name="above")
        factors = keep.tile([P, 2, weight_cols], F32, name="factors")
        ln_factors = keep.tile([P, 2, weight_cols], F32, name="ln_factors")
        ln_weight = keep.tile([P, weight_cols], F32, name="ln_weight")
        nc.vector.scalar_tensor_tensor(
            out=by_slot(magnitude[:]), in0=weights, scalar=-1.0, in1=weights, op0=ALU.mult, op1=ALU.max
        )
        nc.vector.tensor_scalar(
            out=by_slot(half_sign[:]), in0=weights, scalar1=0.0, scalar2=0.5, op0=ALU.is_ge, op1=ALU.subtract
        )
        nc.vector.tensor_scalar(
            out=below[:], in0=magnitude[:], scalar1=LN_LOW, scalar2=LN_HIGH, op0=ALU.min, op1=ALU.mult
        )
        nc.vector.tensor_scalar(
            out=above[:], in0=magnitude[:], scalar1=LN_HIGH, scalar2=LN_LOW, op0=ALU.max, op1=ALU.mult
        )
        nc.vector.tensor_scalar(
            out=factors[:, 0, :], in0=magnitude[:], scalar1=LN_LOW, scalar2=LN_HIGH, op0=ALU.max, op1=ALU.min
        )
        nc.vector.scalar_tensor_tensor(
            out=factors[:, 1, :], in0=below[:], scalar=LN_LOW, in1=above[:], op0=ALU.max, op1=ALU.mult
        )
        nc.scalar.activation(out=ln_factors[:], in_=factors[:], func=ACT.Ln)
        nc.vector.tensor_tensor(out=ln_weight[:], in0=ln_factors[:, 0, :], in1=ln_factors[:, 1, :], op=ALU.add)

        def times_read_sign(name, columns, dtype):
            signed = keep.tile([P, feature_cols], dtype, name=name)
            nc.vector.scalar_tensor_tensor(
                out=by_slot(signed[:]), in0=by_slot(half_sign[:, token_cols:weight_cols]), scalar=2.0,
                in1=columns, op0=ALU.mult, op1=ALU.mult,
            )
            return signed

        def new_grouped(tag, bufs):
            return work.tile([P, W * SLOTS], BF16, tag=tag, name=tag, bufs=bufs, align_bytes=64)

        def new_side():
            return new_grouped("side", 1)

        def in_runs(rows, grouped, first, last):
            source = rows[:, :, first:last].rearrange("p j (c i) -> p c j i", i=RUN)
            target = grouped[:, first * SLOTS : last * SLOTS].rearrange("p (c i j) -> p c j i", i=RUN, j=SLOTS)
            return source, target

        def interleave(rows, grouped, first=0):
            source, target = in_runs(rows, grouped, first, W)
            nc.vector.tensor_copy(out=target, in_=source)

        def move_on_gpsimd(target, source):
            nc.gpsimd.tensor_scalar(out=target, in0=source, scalar1=1.0, scalar2=1.0, op0=ALU.mult, op1=ALU.mult)

        def interleave_on_gpsimd(rows, grouped, last):
            move_on_gpsimd(
                grouped[:, : last * SLOTS].rearrange("p (w j) -> p w j", j=SLOTS),
                rows[:, :, :last].rearrange("p j w -> p w j"),
            )

        def quantize(grouped, tag, bufs):
            codes = work.tile([P, W], U32, tag=tag + "_codes", name=tag + "_codes", bufs=bufs, align_bytes=64)
            scales = work.tile([P, W], U8, tag=tag + "_scales", name=tag + "_scales", bufs=bufs, align_bytes=64)
            nc.vector.quantize_mx(out=codes[:].bitcast(FP8X4), scales=scales[:], in_=grouped[:])
            return codes, scales

        def matmul_pass(bank, stationary, tile_index, moving, start, stop):
            columns = slice(tile_index * P, (tile_index + 1) * P)
            nc.tensor.matmul_mx(
                out=bank[:],
                lhsT=stationary[0][:, columns].bitcast(FP8X4),
                lhsT_scale=stationary[1][:, columns],
                rhs=moving[0][:].bitcast(FP8X4),
                rhs_scale=moving[1][:],
                start=start,
                stop=stop,
            )

        pk_mx, value_mx, query_mx, pq_mx, state_mx = {}, {}, {}, {}, {}
        fresh_banks, query_grouped, pq_rows, pq_grouped = {}, {}, {}, {}

        def sign_value(c):
            for j in range(SLOTS):
                col = c * SLOTS + j
                nc.vector.tensor_scalar(
                    out=values[c][:, j, :], in0=values[c][:, j, :], scalar1=half_sign[:, col : col + 1],
                    scalar2=2.0, op0=ALU.mult, op1=ALU.mult,
                )

        def column_pieces(step):
            width = W // 2 if step == 0 else W
            return [(first, first + width) for first in range(0, W, width)]

        def key_exps(step):
            g, c = divmod(step, TOKEN_PASSES)
            features = work.tile([P, SLOTS, W], F32, tag="key_features", name="key_features", bufs=3)
            for first, last in column_pieces(step):
                tiles = slice(first // P, last // P)
                for j in range(SLOTS):
                    col = c * SLOTS + j
                    nc.scalar.activation(
                        out=features[:, j, :].rearrange("p (t m) -> p t m", t=SLOTS)[:, tiles],
                        in_=keys[c][:, j, :].rearrange("p (m t) -> p t m", t=SLOTS)[:, tiles],
                        func=ACT.Exp, scale=1.0 - 2.0 * g, bias=ln_weight[:, col : col + 1],
                    )
            return features

        def times_key_gain(step, features):
            g = step // TOKEN_PASSES
            grouped = new_grouped("pk_grouped", 2)
            for first, last in column_pieces(step):
                source, target = in_runs(features, grouped, first, last)
                gains = gain_bank[:, g * W + first : g * W + last].rearrange("p (c i) -> p c i", i=RUN)
                gains = gains.unsqueeze(2).to_broadcast([P, (last - first) // RUN, SLOTS, RUN])
                nc.vector.tensor_tensor(out=target, in0=source, in1=gains, op=ALU.mult)
            return grouped

        def fresh_passes(step):
            g, c = divmod(step, TOKEN_PASSES)
            for t in range(SLOTS):
                if c == 0:
                    fresh_banks[g, t] = psum.tile([P, E], F32, tag="sum%d" % t, name="fresh_bank")
                matmul_pass(fresh_banks[g, t], pk_mx[step], t, value_mx[c], c == 0, c == TOKEN_PASSES - 1)

        def updated_state_rows(g):
            rows = work.tile([P, SLOTS, E], BF16, tag="state_rows", name="state_rows", bufs=HALVES)
            for t in range(SLOTS):
                col = g * SLOTS + t
                nc.vector.scalar_tensor_tensor(
                    out=rows[:, t, :], in0=states[g][:, t, :], scalar=signed_decay[:, col : col + 1],
                    in1=fresh_banks[g, t][:], op0=ALU.mult, op1=ALU.add,
                )
            return rows

        def transpose_queries(index, tag):
            n, h = divmod(index, 2)
            if h == 0:
                query_grouped[n] = new_grouped("query_grouped", 2)
            bank = psum.tile([P, 2, 2, P], F32, tag=tag, name="turn_bank")
            for b in range(2):
                words = queries[n][:, 2 * h + b, :].bitcast(F32)
                for u in range(2):
                    nc.tensor.transpose(bank[:, b, u, :], words[:, u : 2 * P : 2], identity_f32[:])
            return bank

        def copy_queries(index, bank):
            n, h = divmod(index, 2)
            words = query_grouped[n][:, h * 2 * W : (h + 1) * 2 * W].bitcast(F32)
            nc.scalar.copy(
                out=words.rearrange("p (b r u) -> p b r u", b=2, u=2), in_=bank[:].rearrange("p b u r -> p b r u")
            )

        def project_slot(n, t, tag):
            bank = psum.tile([P, W], F32, tag=tag, name="projection_bank")
            matmul_pass(bank, omega_mx, t, query_mx[n], True, True)
            return bank

        def project(part, tags=("project0", "project1")):
            n, h = divmod(part, 2)
            return [project_slot(n, 2 * h + k, tags[k]) for k in range(2)]

        def query_exps(part, banks):
            n, h = divmod(part, 2)
            if h == 0:
                for g in range(HALVES):
                    pq_rows[n, g] = work.tile([P, SLOTS, W], BF16, tag="pq_rows", name="pq_rows", bufs=GROUPS * HALVES)
            for k in range(2):
                t = 2 * h + k
                for g in range(HALVES):
                    col = token_cols + g * SLOTS + t
                    nc.scalar.activation(
                        out=pq_rows[n, g][:, t, :], in_=banks[k][:], func=ACT.Exp,
                        scale=1.0 - 2.0 * g, bias=ln_weight[:, col : col + 1],
                    )

        def quantize_pq(n, g, grouped):
            pq_mx[n, g] = quantize(grouped, "pq", GROUPS * HALVES)

        sign_value(0)
        value_grouped = new_side()
        signed_gain = times_read_sign("signed_gain", key_gains, BF16)
        interleave(values[0], value_grouped)
        gain_bank = psum.tile([P, F], BF16, tag="gain", name="gain_bank")
        for col in range(feature_cols):
            nc.tensor.transpose(
                gain_bank[:, col * P : (col + 1) * P],
                signed_gain[:, col : col + 1].to_broadcast([P, P]),
                identity_bf16[:],
            )
        value_mx[0] = quantize(value_grouped, "value", TOKEN_PASSES)

        update_step = TOKEN_PASSES - 1 + FRESH_LAG
        next_turn = next_part = 0
        for step in range(STEPS):
            projects = step >= QUERY_START and step != QUERY_PAUSE
            turn_count = 0 if step == 1 else 1 if projects else 2
            turns = range(next_turn, min(next_turn + turn_count, 2 * GROUPS))
            next_turn = turns.stop
            turn_banks = [transpose_queries(index, tag) for index, tag in zip(turns, ("turn", "project0"))]
            if projects:
                projection_banks = project(next_part)
            if step >= FRESH_LAG:
                fresh_passes(step - FRESH_LAG)

            features = key_exps(step)
            for index, bank in zip(turns, turn_banks):
                copy_queries(index, bank)
            if projects:
                query_exps(next_part, projection_banks)
                next_part = next_part + 1

            side = new_side()
            pk_grouped = times_key_gain(step, features)
            if step == 0:
                target = side[:].rearrange("p (t m j) -> p t m j", t=SLOTS, j=SLOTS)
                source = omega_rows[:].rearrange("p j (m t) -> p t m j", t=SLOTS)
                move_on_gpsimd(target[:, : SLOTS - 1], source[:, : SLOTS - 1])
                nc.vector.tensor_copy(out=target[:, SLOTS - 1], in_=source[:, SLOTS - 1])
            elif step == update_step:
                interleave_on_gpsimd(pq_rows[0, 1], side, W)
                state_rows = updated_state_rows(0)
            else:
                if step < TOKEN_PASSES:
                    side_rows = values[step]
                elif step < update_step:
                    side_rows = pq_rows[0, 0]
                elif step == update_step + 1:
                    side_rows = state_rows
                else:
                    side_rows = pq_rows[1, 0]
                interleave_on_gpsimd(side_rows, side, GPSIMD_COLUMNS)
                interleave(side_rows, side, GPSIMD_COLUMNS)
            if step == update_step - 1:
                signed_decay = times_read_sign("signed_decay", decays, F32)
            if step + 1 < TOKEN_PASSES:
                sign_value(step + 1)
            for index in turns:
                if index % 2 == 1:
                    query_mx[index // 2] = quantize(query_grouped[index // 2], "query", 2)
            if step == 0:
                omega_mx = quantize(side, "omega", 1)
            elif step < TOKEN_PASSES:
                value_mx[step] = quantize(side, "value", TOKEN_PASSES)
            elif step <= update_step:
                quantize_pq(0, step - TOKEN_PASSES, side)
            elif step == update_step + 1:
                state_mx[0] = quantize(side, "state", HALVES)
            pk_mx[step] = quantize(pk_grouped, "pk", FRESH_LAG + 2)

        last_group = GROUPS - 1
        projection_banks = [project_slot(last_group - 1, 2, "project0")]
        fresh_passes(STEPS - 2)
        projection_banks.append(project_slot(last_group - 1, 3, "project1"))
        first_slot_bank = project_slot(last_group, 0, "turn")
        query_exps(next_part, projection_banks)
        fresh_passes(STEPS - 1)
        query_exps(2 * last_group, [first_slot_bank, project_slot(last_group, 1, "project0")])
        query_exps(2 * last_group + 1, project(2 * last_group + 1, ("project1", "turn")))

        def reuse_value_tile(c):
            return keep.tile([P, W * SLOTS], BF16, tag="value%d" % c, name="late_grouped", align_bytes=64)

        quantize_pq(1, 0, side)
        pq_grouped[2, 1] = new_side()
        interleave_on_gpsimd(pq_rows[2, 1], pq_grouped[2, 1], GPSIMD_COLUMNS)
        pq_grouped[1, 1] = reuse_value_tile(3)
        interleave(pq_rows[1, 1], pq_grouped[1, 1])
        state_rows = updated_state_rows(1)
        state_grouped = reuse_value_tile(0)
        interleave(state_rows, state_grouped)
        interleave(pq_rows[2, 1], pq_grouped[2, 1], GPSIMD_COLUMNS)
        state_mx[1] = quantize(state_grouped, "state", HALVES)

        pq_grouped[2, 0] = reuse_value_tile(1)
        interleave(pq_rows[2, 0], pq_grouped[2, 0])
        quantize_pq(1, 1, pq_grouped[1, 1])
        pq_grouped[3, 0] = reuse_value_tile(2)
        source, target = in_runs(pq_rows[3, 0], pq_grouped[3, 0], 0, SCALAR_COLUMNS)
        nc.scalar.copy(out=target, in_=source)
        interleave(pq_rows[3, 0], pq_grouped[3, 0], SCALAR_COLUMNS)
        quantize_pq(2, 0, pq_grouped[2, 0])
        quantize_pq(2, 1, pq_grouped[2, 1])
        pq_grouped[3, 1] = new_side()
        interleave_on_gpsimd(pq_rows[3, 1], pq_grouped[3, 1], W)
        quantize_pq(3, 0, pq_grouped[3, 0])

        root_scale = keep.tile([P, 1], F32, name="root_scale")
        nc.scalar.activation(out=root_scale[:], in_=row_length[:], func=ACT.Abs_reciprocal_sqrt)
        bank_tags = ["sum0", "sum1", "sum2", "sum3", "gain", "turn", "project0", "project1"]
        mean_square = keep.tile([P, 2 * PAIRS], F32, name="mean_square")
        inverse_rms = keep.tile([P, 2 * PAIRS], F32, name="inverse_rms")
        read_banks = {}

        def read_pass(tile_index, g):
            n, b = divmod(tile_index, SLOTS)
            if g == 0:
                tag = bank_tags[tile_index % len(bank_tags)]
                read_banks[tile_index] = psum.tile([P, E], F32, tag=tag, name="read_bank")
            matmul_pass(read_banks[tile_index], pq_mx[n, g], b, state_mx[g], g == 0, g == HALVES - 1)

        def sum_squares(tile_index):
            squares = work.tile([P, E], BF16, tag="squares", name="squares", bufs=2)
            nc.scalar.activation(
                out=squares[:], in_=read_banks[tile_index][:], func=ACT.Square, scale=root_scale[:],
                accum_out=mean_square[:, tile_index : tile_index + 1],
            )

        def invert_rms(pair):
            columns = slice(2 * pair, 2 * pair + 2)
            nc.scalar.activation(
                out=inverse_rms[:, columns], in_=mean_square[:, columns], func=ACT.Abs_reciprocal_sqrt, bias=EPS
            )

        def finish(pair):
            n, h = divmod(pair, 2)
            rows = out[n * W : (n + 1) * W, :].rearrange("(r b) e -> r b e", b=SLOTS)
            by_tile = pair in (0, PAIRS - 1)
            result = work.tile([P, 2, E], F32, tag="result", name="result", bufs=5)
            for b in range(2):
                tile_index = 2 * pair + b
                nc.vector.scalar_tensor_tensor(
                    out=result[:, b, :], in0=read_banks[tile_index][:],
                    scalar=inverse_rms[:, tile_index : tile_index + 1], in1=gain_row[:],
                    op0=ALU.mult, op1=ALU.mult,
                )
                if by_tile:
                    nc.sync.dma_start(out=rows[:, 2 * h + b, :], in_=result[:, b, :])
            if not by_tile:
                nc.sync.dma_start(out=rows[:, 2 * h : 2 * h + 2, :], in_=result[:])

        for tile_index in range(EARLY_READS):
            read_pass(tile_index, 0)
        for pair in range(PAIRS + 1):
            if pair < PAIRS:
                for tile_index in (2 * pair, 2 * pair + 1):
                    if tile_index >= EARLY_READS:
                        read_pass(tile_index, 0)
                    read_pass(tile_index, 1)
                sum_squares(2 * pair)
            if pair >= 1:
                invert_rms(pair - 1)
            if pair < PAIRS:
                sum_squares(2 * pair + 1)
            if pair >= 1:
                finish(pair - 1)
            if pair == GPSIMD_PAIRS:
                quantize_pq(3, 1, pq_grouped[3, 1])
